import numpy as np
import ml_dtypes


def mxq(x, axis, fmt="e4m3"):
    dtype, down = {"e4m3": (ml_dtypes.float8_e4m3fn, 7), "e5m2": (ml_dtypes.float8_e5m2, 14)}[fmt]
    v = np.moveaxis(np.asarray(x, np.float32).astype(ml_dtypes.bfloat16).astype(np.float64), axis, -1)
    blocks = v.reshape(v.shape[:-1] + (-1, 32))
    amax = np.abs(blocks).max(-1, keepdims=True)
    byte = np.maximum(np.where(amax > 0, np.frexp(amax)[1] - 1 + 127, 0) - down, 1)
    scale = np.exp2(byte - 127.0)
    codes = (blocks / scale).astype(np.float32).astype(dtype).astype(np.float64)
    return np.moveaxis((codes * scale).reshape(v.shape), -1, axis)


WIDE = False


def mx_kscale(k):
    if not WIDE:
        return np.ones(k)
    levels = np.array([10, -10, 5, -5, 0])
    if k % 512:
        return np.exp2(np.random.permutation(np.resize(levels, k // 32))).repeat(32)
    a = np.empty((k // 512, 16))
    for p in range(k // 512):
        a[p, :8] = np.random.permutation(np.resize(levels, 8))
        for g in range(8):
            far = levels[np.abs(levels - a[p, g]) >= 10]
            a[p, g + 8] = far[np.random.randint(len(far))]
    return np.exp2(a.ravel()).repeat(32)


def f64(x):
    return np.asarray(x).astype(np.float64)


def striped8(idx):
    return np.concatenate([v.reshape(-1, 16).T for v in idx]).astype(np.uint16)


def unstriped8(offs):
    return np.stack([offs[16 * g:16 * g + 16].T.reshape(-1) for g in range(8)]).astype(np.int64)


def silu(v):
    return v / (1.0 + np.exp(-np.maximum(v, -700.0)))


K, M, T, S = 512, 256, 2048, 1024


def setup_inputs():
    n = np.random.standard_normal
    s = mx_kscale(K)[:, None]
    return {
        "xT": (n((K, T)) * s).astype(np.float32),
        "w": (n((K, M)) / np.sqrt(K) / s).astype(np.float32),
        "wgt": np.repeat(np.random.uniform(0.5, 2.0, (8, S)), 16, axis=0).astype(np.float32),
        "b": (0.3 * n(256)).astype(np.float32),
        "wgo": np.repeat(np.random.uniform(0.5, 2.0, (8, S)), 16, axis=0).astype(np.float32),
        "offs": striped8(np.stack([np.random.permutation(T)[:S] for _ in range(8)])),
        "offs2": striped8(np.stack([np.random.permutation(T)[:S] for _ in range(8)])),
    }


def reference(xT, w, wgt, b, wgo, offs, offs2):
    idx = unstriped8(offs)
    group = np.arange(K) % 512 // 64
    xg = f64(wgt)[np.arange(K) // 4 % 128] * f64(xT)[np.arange(K)[:, None], idx[group]]
    xT_ = mxq(xg, 0, "e4m3")
    w_ = mxq(f64(w), 0, "e4m3")
    y = w_.T @ xT_
    place = unstriped8(offs2)[np.arange(M) % 128 // 16]
    out = np.zeros((M, T))
    out[np.arange(M)[:, None], place] = f64(wgo)[np.arange(M) % 128] * (silu(y + f64(b)[:, None]))
    return out

@@ -1,0 +1,157 @@
+from contextlib import ExitStack
+
+import concourse.mybir as mybir
+
+K, M, T, S = 512, 256, 2048, 1024
+FLOPS = 2 * K * M * S
+
+F32 = mybir.dt.float32
+BF16 = mybir.dt.bfloat16
+U32 = mybir.dt.uint32
+U16 = mybir.dt.uint16
+U8 = mybir.dt.uint8
+FP8X4 = mybir.dt.float8_e4m3fn_x4
+MULT = mybir.AluOpType.mult
+SILU = mybir.ActivationFunctionType.Silu
+
+P = 128
+PACK = 4
+HALF = S // 2
+LIST_ROWS = 16
+
+
+def tile_list_hboth_silu_kernel(tc, xT, w, wgt, b, wgo, offs, offs2, out):
+    nc = tc.nc
+    with ExitStack() as ctx:
+        keep = ctx.enter_context(tc.tile_pool(name="keep", bufs=1))
+        psum = ctx.enter_context(tc.psum_pool(name="psum", bufs=1))
+
+        offs_t = keep.tile([P, S // LIST_ROWS], U16, name="offs_t")
+        offs2_t = keep.tile([P, S // LIST_ROWS], U16, name="offs2_t")
+        planes = [keep.tile([P, T], F32, name=f"plane{i}") for i in range(PACK)]
+        wgt_t = keep.tile([P, S], F32, name="wgt_t")
+        w_raw = keep.tile([P, PACK, M], F32, name="w_raw")
+        wgo_t = keep.tile([P, S], F32, name="wgo_t")
+        b_t = keep.tile([P, 2], F32, name="b_t")
+        picked = [keep.tile([P, PACK, HALF], F32, name=f"picked{h}") for h in range(2)]
+        grouped = [keep.tile([P, HALF, PACK], BF16, name=f"grouped{h}", align_bytes=64) for h in range(2)]
+        codes = [keep.tile([P, HALF], U32, name=f"codes{h}", align_bytes=64) for h in range(2)]
+        scales = [keep.tile([P, HALF], U8, name=f"scales{h}", align_bytes=64) for h in range(2)]
+        w_grouped = [keep.tile([P, P, PACK], BF16, name=f"w_grouped{r}", align_bytes=64) for r in range(2)]
+        w_codes = [keep.tile([P, P], U32, name=f"w_codes{r}", align_bytes=64) for r in range(2)]
+        w_scales = [keep.tile([P, P], U8, name=f"w_scales{r}", align_bytes=64) for r in range(2)]
+        windows = [keep.tile([P, T], F32, name=f"window{r}") for r in range(2)]
+        y = [[keep.tile([P, HALF], F32, name=f"y{r}{h}") for h in range(2)] for r in range(2)]
+        warm = keep.tile([P, 1], F32, name="warm")
+
+        x_planes = xT.rearrange("(p i) t -> p i t", i=PACK)
+        nc.sync.dma_start(offs_t[:], offs)
+        nc.sync.dma_start(wgt_t[:, 0:P], wgt[:, 0:P])
+        nc.sync.dma_start(planes[0][:], x_planes[:, 0, :])
+        nc.sync.dma_start(wgt_t[:, P:HALF], wgt[:, P:HALF])
+        nc.sync.dma_start(wgt_t[:, HALF:S], wgt[:, HALF:S])
+        for i in range(1, PACK):
+            nc.sync.dma_start(planes[i][:], x_planes[:, i, :])
+        nc.sync.dma_start(w_raw[:], w.rearrange("(p i) m -> p i m", i=PACK))
+        nc.sync.dma_start(offs2_t[:], offs2)
+        nc.sync.dma_start(wgo_t[:, 0:HALF], wgo[:, 0:HALF])
+        with nc.allow_non_contiguous_dma(reason="bias, one value to a partition"):
+            nc.sync.dma_start(b_t[:], b.rearrange("(r p) -> p r", p=P))
+        nc.sync.dma_start(wgo_t[:, HALF:S], wgo[:, HALF:S])
+
+        nc.vector.memset(warm[:], 0.0)
+        nc.scalar.activation(warm[:], warm[:], SILU)
+        nc.vector.memset(windows[0][:], 0.0)
+        nc.gpsimd.memset(windows[1][:], 0.0)
+
+        def gather(i, h, c0, c1):
+            j0, j1 = h * HALF + c0, h * HALF + c1
+            nc.vector.tensor_tensor(
+                picked[h][:, i, c0:c1],
+                planes[i][:].indirect(offs_t[:, j0 // LIST_ROWS : j1 // LIST_ROWS]),
+                wgt_t[:, j0:j1],
+                MULT,
+            )
+
+        def interleave(copy, pair, h, c0, c1):
+            i0 = 2 * pair
+            copy(
+                grouped[h][:, c0:c1, i0 : i0 + 2],
+                picked[h][:, i0 : i0 + 2, c0:c1].rearrange("p i n -> p n i"),
+            )
+
+        def quantize(h, c0, c1):
+            nc.vector.quantize_mx(
+                out=codes[h][:, c0:c1].bitcast(FP8X4),
+                scales=scales[h][:, c0:c1],
+                in_=grouped[h][:, c0:c1, :].rearrange("p n i -> p (n i)"),
+            )
+
+        def interleave_w(copy, r):
+            copy(w_grouped[r][:], w_raw[:, :, r * P : (r + 1) * P].rearrange("p i m -> p m i"))
+
+        def quantize_w(r):
+            nc.vector.quantize_mx(
+                out=w_codes[r][:].bitcast(FP8X4),
+                scales=w_scales[r][:],
+                in_=w_grouped[r][:].rearrange("p m i -> p (m i)"),
+            )
+
+        def product(r, h, c0, c1):
+            bank = psum.tile([P, c1 - c0], F32, name=f"bank{r}_{h}_{c0}")
+            nc.tensor.matmul_mx(
+                out=bank[:],
+                lhsT=w_codes[r][:].bitcast(FP8X4),
+                lhsT_scale=w_scales[r][:],
+                rhs=codes[h][:, c0:c1].bitcast(FP8X4),
+                rhs_scale=scales[h][:, c0:c1],
+                start=True,
+                stop=True,
+            )
+            nc.scalar.activation(y[r][h][:, c0:c1], bank[:], SILU, bias=b_t[:, r : r + 1])
+
+        def scatter(r, h):
+            cols = slice(h * HALF, (h + 1) * HALF)
+            nc.vector.tensor_tensor(
+                windows[r][:].indirect(offs2_t[:, h * HALF // LIST_ROWS : (h + 1) * HALF // LIST_ROWS]),
+                y[r][h][:],
+                wgo_t[:, cols],
+                MULT,
+            )
+
+        Q = HALF // 2
+        for i in range(3):
+            for h in range(2):
+                if i == 0 and h == 0:
+                    gather(i, h, 0, P)
+                    gather(i, h, P, HALF)
+                else:
+                    gather(i, h, 0, HALF)
+                if i == 1:
+                    interleave(nc.scalar.copy, 0, h, 0, HALF)
+        gather(3, 0, 0, Q)
+        interleave(nc.scalar.copy, 1, 0, 0, Q)
+        gather(3, 0, Q + P, HALF)
+        gather(3, 0, Q, Q + P)
+        interleave(nc.scalar.copy, 1, 0, Q, Q + P)
+        interleave(nc.vector.tensor_copy, 1, 0, Q + P, HALF)
+        interleave_w(nc.vector.tensor_copy, 0)
+        quantize(0, 0, Q)
+        quantize_w(0)
+        interleave_w(nc.scalar.copy, 1)
+        quantize(0, Q, HALF)
+        product(0, 0, 0, Q)
+        product(0, 0, Q, HALF)
+        gather(3, 1, 0, HALF)
+        quantize_w(1)
+        product(1, 0, 0, Q)
+        product(1, 0, Q, HALF)
+        interleave(nc.scalar.copy, 1, 1, 0, HALF)
+        scatter(0, 0)
+        quantize(1, 0, HALF)
+        for r in range(2):
+            product(r, 1, 0, HALF)
+        scatter(1, 0)
+        for r in range(2):
+            scatter(r, 1)
+            nc.sync.dma_start(out[r * P : (r + 1) * P, :], windows[r][:])

@@ -1,6 +1,7 @@
 from contextlib import ExitStack
 
 import concourse.mybir as mybir
+from concourse.masks import make_identity
 
 K, M, T, S = 512, 256, 2048, 1024
 FLOPS = 2 * K * M * S
@@ -17,7 +18,12 @@ SILU = mybir.ActivationFunctionType.Silu
 P = 128
 PACK = 4
 HALF = S // 2
+QUARTER = S // 4
 LIST_ROWS = 16
+HEADS = P // LIST_ROWS
+SPREAD = ((0, 128), (128, 256), (256, 512), (512, 768), (768, 1024))
+BANK = ((7, 7), (1, 1), (2, 3), (4, 5))
+PIECES = ((768, 1024), (0, 256), (256, 512), (512, 768))
 
 
 def tile_list_hboth_silu_kernel(tc, xT, w, wgt, b, wgo, offs, offs2, out):
@@ -30,128 +36,168 @@ def tile_list_hboth_silu_kernel(tc, xT, w, wgt, b, wgo, offs, offs2, out):
         offs2_t = keep.tile([P, S // LIST_ROWS], U16, name="offs2_t")
         planes = [keep.tile([P, T], F32, name=f"plane{i}") for i in range(PACK)]
         wgt_t = keep.tile([P, S], F32, name="wgt_t")
-        w_raw = keep.tile([P, PACK, M], F32, name="w_raw")
         wgo_t = keep.tile([P, S], F32, name="wgo_t")
         b_t = keep.tile([P, 2], F32, name="b_t")
-        picked = [keep.tile([P, PACK, HALF], F32, name=f"picked{h}") for h in range(2)]
-        grouped = [keep.tile([P, HALF, PACK], BF16, name=f"grouped{h}", align_bytes=64) for h in range(2)]
-        codes = [keep.tile([P, HALF], U32, name=f"codes{h}", align_bytes=64) for h in range(2)]
-        scales = [keep.tile([P, HALF], U8, name=f"scales{h}", align_bytes=64) for h in range(2)]
-        w_grouped = [keep.tile([P, P, PACK], BF16, name=f"w_grouped{r}", align_bytes=64) for r in range(2)]
+        picked_row = keep.tile([P, PACK * S], F32, name="picked_row", align_bytes=64)
+        picked = picked_row[:].rearrange("p (i n) -> p i n", i=PACK)
+        late = [keep.tile([P, HALF], F32, name=f"late{r}", align_bytes=64) for r in range(2)]
+        grouped = [keep.tile([P, (c1 - c0) * PACK], BF16, name=f"grouped{c0}", align_bytes=64)[:] for c0, c1 in PIECES[:2]]
+        grouped = grouped + [late[r][:].bitcast(BF16) for r in range(2)]
+        codes = [keep.tile([P, c1 - c0], U32, name=f"codes{c0}", align_bytes=64) for c0, c1 in PIECES]
+        scales = [keep.tile([P, c1 - c0], U8, name=f"scales{c0}", align_bytes=64) for c0, c1 in PIECES]
+        w_grouped = [picked_row[:, 3 * S + (r - 1) * QUARTER : 3 * S + r * QUARTER].bitcast(BF16) for r in range(2)]
         w_codes = [keep.tile([P, P], U32, name=f"w_codes{r}", align_bytes=64) for r in range(2)]
         w_scales = [keep.tile([P, P], U8, name=f"w_scales{r}", align_bytes=64) for r in range(2)]
         windows = [keep.tile([P, T], F32, name=f"window{r}") for r in range(2)]
-        y = [[keep.tile([P, HALF], F32, name=f"y{r}{h}") for h in range(2)] for r in range(2)]
+        y_second = [keep.tile([P, QUARTER], F32, name=f"y_second{r}") for r in range(2)]
+        y_last = [keep.tile([P, HALF], F32, name=f"y_last{r}") for r in range(2)]
+        y = [
+            [
+                late[r][:, 0:QUARTER],
+                y_second[r][:],
+                y_last[r][:, 0:QUARTER],
+                y_last[r][:, QUARTER:HALF],
+            ]
+            for r in range(2)
+        ]
         warm = keep.tile([P, 1], F32, name="warm")
+        ident = keep.tile([P, P], F32, name="ident")
+        rows = keep.tile([P, P], F32, name="rows")
+        spread = keep.tile([P, S], F32, name="spread")
+        w_raw = keep.tile([P, PACK, M], F32, name="w_raw")
 
         x_planes = xT.rearrange("(p i) t -> p i t", i=PACK)
+        nc.sync.dma_start(rows[0:64, :], wgt[0:P:LIST_ROWS, :].rearrange("g (b c) -> b g c", c=P))
         nc.sync.dma_start(offs_t[:], offs)
-        nc.sync.dma_start(wgt_t[:, 0:P], wgt[:, 0:P])
-        nc.sync.dma_start(planes[0][:], x_planes[:, 0, :])
-        nc.sync.dma_start(wgt_t[:, P:HALF], wgt[:, P:HALF])
-        nc.sync.dma_start(wgt_t[:, HALF:S], wgt[:, HALF:S])
-        for i in range(1, PACK):
+        for i in range(PACK):
             nc.sync.dma_start(planes[i][:], x_planes[:, i, :])
-        nc.sync.dma_start(w_raw[:], w.rearrange("(p i) m -> p i m", i=PACK))
-        nc.sync.dma_start(offs2_t[:], offs2)
-        nc.sync.dma_start(wgo_t[:, 0:HALF], wgo[:, 0:HALF])
-        with nc.allow_non_contiguous_dma(reason="bias, one value to a partition"):
-            nc.sync.dma_start(b_t[:], b.rearrange("(r p) -> p r", p=P))
-        nc.sync.dma_start(wgo_t[:, HALF:S], wgo[:, HALF:S])
 
         nc.vector.memset(warm[:], 0.0)
         nc.scalar.activation(warm[:], warm[:], SILU)
+        make_identity(nc, ident[:])
+        nc.gpsimd.memset(rows[64:P, :], 0.0)
         nc.vector.memset(windows[0][:], 0.0)
         nc.gpsimd.memset(windows[1][:], 0.0)
 
-        def gather(i, h, c0, c1):
-            j0, j1 = h * HALF + c0, h * HALF + c1
+        turned = [psum.tile([P, P], F32, name=f"turned{e}", tag=f"bk{e}") for e in range(2)]
+        for e in range(2):
+            nc.tensor.transpose(turned[e][:], rows[:], ident[:])
+
+        def expand(copy, e, c0, c1):
+            copy(
+                spread[:, c0:c1].rearrange("j (k q) -> j k q", q=LIST_ROWS),
+                turned[e][:, c0 // LIST_ROWS : c1 // LIST_ROWS].unsqueeze(2).to_broadcast([P, (c1 - c0) // LIST_ROWS, LIST_ROWS]),
+            )
+
+        expand(nc.scalar.copy, 1, HALF, S)
+        for n, (c0, c1) in enumerate(SPREAD):
+            if c0 < HALF:
+                expand(nc.vector.tensor_copy, 0, c0, c1)
+            back = psum.tile([P, c1 - c0], F32, name=f"back{n}", tag=f"bk{n + 2}")
+            for c in range(0, c1 - c0, P):
+                nc.tensor.transpose(back[:, c : c + P], spread[:, c0 + c : c0 + c + P], ident[:])
+            nc.scalar.copy(wgt_t[:, c0:c1], back[:])
+
+        nc.sync.dma_start(w_raw[:], w.rearrange("(p i) m -> p i m", i=PACK))
+        with nc.allow_non_contiguous_dma(reason="bias, one value to a partition"):
+            nc.sync.dma_start(b_t[:], b.rearrange("(r p) -> p r", p=P))
+        nc.sync.dma_start(offs2_t[:], offs2)
+        nc.sync.dma_start(wgo_t[:, 3 * QUARTER : S], wgo[:, 3 * QUARTER : S])
+        nc.sync.dma_start(wgo_t[:, 0 : 3 * QUARTER], wgo[:, 0 : 3 * QUARTER])
+
+        def gather(i, c0, c1):
             nc.vector.tensor_tensor(
-                picked[h][:, i, c0:c1],
-                planes[i][:].indirect(offs_t[:, j0 // LIST_ROWS : j1 // LIST_ROWS]),
-                wgt_t[:, j0:j1],
+                picked_row[:, i * S + c0 : i * S + c1],
+                planes[i][:].indirect(offs_t[:, c0 // LIST_ROWS : c1 // LIST_ROWS]),
+                wgt_t[:, c0:c1],
                 MULT,
             )
 
-        def interleave(copy, pair, h, c0, c1):
-            i0 = 2 * pair
-            copy(
-                grouped[h][:, c0:c1, i0 : i0 + 2],
-                picked[h][:, i0 : i0 + 2, c0:c1].rearrange("p i n -> p n i"),
+        def interleave(pair, n, c0, c1):
+            first = PIECES[n][0]
+            nc.scalar.copy(
+                grouped[n].rearrange("p (n i) -> p n i", i=PACK)[:, c0 - first : c1 - first, 2 * pair : 2 * pair + 2],
+                picked[:, 2 * pair : 2 * pair + 2, c0:c1].rearrange("p i n -> p n i"),
             )
 
-        def quantize(h, c0, c1):
+        def interleave_all(n):
+            c0, c1 = PIECES[n]
+            nc.scalar.copy(
+                grouped[n].rearrange("p (c j i) -> p c i j", j=4, i=PACK),
+                picked[:, :, c0:c1].rearrange("p i (c j) -> p c i j", j=4),
+            )
+
+        def quantize(n):
             nc.vector.quantize_mx(
-                out=codes[h][:, c0:c1].bitcast(FP8X4),
-                scales=scales[h][:, c0:c1],
-                in_=grouped[h][:, c0:c1, :].rearrange("p n i -> p (n i)"),
+                out=codes[n][:].bitcast(FP8X4),
+                scales=scales[n][:],
+                in_=grouped[n],
             )
 
-        def interleave_w(copy, r):
-            copy(w_grouped[r][:], w_raw[:, :, r * P : (r + 1) * P].rearrange("p i m -> p m i"))
+        def interleave_w(r):
+            nc.scalar.copy(
+                w_grouped[r].rearrange("p (c j i) -> p c i j", j=4, i=PACK),
+                w_raw[:, :, r * P : (r + 1) * P].rearrange("p i (c j) -> p c i j", j=4),
+            )
 
         def quantize_w(r):
             nc.vector.quantize_mx(
                 out=w_codes[r][:].bitcast(FP8X4),
                 scales=w_scales[r][:],
-                in_=w_grouped[r][:].rearrange("p m i -> p (m i)"),
+                in_=w_grouped[r],
             )
 
-        def product(r, h, c0, c1):
-            bank = psum.tile([P, c1 - c0], F32, name=f"bank{r}_{h}_{c0}")
+        def product(r, n):
+            c0, c1 = PIECES[n]
+            bank = psum.tile([P, c1 - c0], F32, name=f"bank{r}_{n}", tag=f"bk{BANK[n][r]}")
             nc.tensor.matmul_mx(
                 out=bank[:],
                 lhsT=w_codes[r][:].bitcast(FP8X4),
                 lhsT_scale=w_scales[r][:],
-                rhs=codes[h][:, c0:c1].bitcast(FP8X4),
-                rhs_scale=scales[h][:, c0:c1],
+                rhs=codes[n][:].bitcast(FP8X4),
+                rhs_scale=scales[n][:],
                 start=True,
                 stop=True,
             )
-            nc.scalar.activation(y[r][h][:, c0:c1], bank[:], SILU, bias=b_t[:, r : r + 1])
+            nc.scalar.activation(y[r][n], bank[:], SILU, bias=b_t[:, r : r + 1])
 
-        def scatter(r, h):
-            cols = slice(h * HALF, (h + 1) * HALF)
+        def scatter(r, values, c0, c1):
             nc.vector.tensor_tensor(
-                windows[r][:].indirect(offs2_t[:, h * HALF // LIST_ROWS : (h + 1) * HALF // LIST_ROWS]),
-                y[r][h][:],
-                wgo_t[:, cols],
+                windows[r][:].indirect(offs2_t[:, c0 // LIST_ROWS : c1 // LIST_ROWS]),
+                values,
+                wgo_t[:, c0:c1],
                 MULT,
             )
 
-        Q = HALF // 2
-        for i in range(3):
-            for h in range(2):
-                if i == 0 and h == 0:
-                    gather(i, h, 0, P)
-                    gather(i, h, P, HALF)
-                else:
-                    gather(i, h, 0, HALF)
-                if i == 1:
-                    interleave(nc.scalar.copy, 0, h, 0, HALF)
-        gather(3, 0, 0, Q)
-        interleave(nc.scalar.copy, 1, 0, 0, Q)
-        gather(3, 0, Q + P, HALF)
-        gather(3, 0, Q, Q + P)
-        interleave(nc.scalar.copy, 1, 0, Q, Q + P)
-        interleave(nc.vector.tensor_copy, 1, 0, Q + P, HALF)
-        interleave_w(nc.vector.tensor_copy, 0)
-        quantize(0, 0, Q)
+        for c0, c1 in SPREAD:
+            gather(0, c0, c1)
+        gather(1, 0, S)
+        for n in range(2):
+            interleave(0, n, *PIECES[n])
+        gather(2, 0, S)
+        for c in (7 * P, 6 * P):
+            gather(3, c, c + P)
+            interleave(1, 0, c, c + P)
+        gather(3, QUARTER, 3 * QUARTER)
+        interleave_w(0)
+        interleave_w(1)
+        quantize(0)
         quantize_w(0)
-        interleave_w(nc.scalar.copy, 1)
-        quantize(0, Q, HALF)
-        product(0, 0, 0, Q)
-        product(0, 0, Q, HALF)
-        gather(3, 1, 0, HALF)
+        product(0, 0)
         quantize_w(1)
-        product(1, 0, 0, Q)
-        product(1, 0, Q, HALF)
-        interleave(nc.scalar.copy, 1, 1, 0, HALF)
-        scatter(0, 0)
-        quantize(1, 0, HALF)
+        product(1, 0)
+        gather(3, 0, QUARTER)
+        interleave(1, 1, *PIECES[1])
+        scatter(0, y[0][0], *PIECES[0])
+        quantize(1)
+        scatter(1, y[1][0], *PIECES[0])
         for r in range(2):
-            product(r, 1, 0, HALF)
-        scatter(1, 0)
+            interleave_all(2 + r)
+            quantize(2 + r)
+            product(r, 1)
+            scatter(r, y[r][1], *PIECES[1])
         for r in range(2):
-            scatter(r, 1)
+            product(r, 2)
+            product(r, 3)
+            scatter(r, y_last[r][:], QUARTER, 3 * QUARTER)
             nc.sync.dma_start(out[r * P : (r + 1) * P, :], windows[r][:])

@@ -45,7 +45,7 @@ def tile_list_hboth_silu_kernel(tc, xT, w, wgt, b, wgo, offs, offs2, out):
         grouped = grouped + [late[r][:].bitcast(BF16) for r in range(2)]
         codes = [keep.tile([P, c1 - c0], U32, name=f"codes{c0}", align_bytes=64) for c0, c1 in PIECES]
         scales = [keep.tile([P, c1 - c0], U8, name=f"scales{c0}", align_bytes=64) for c0, c1 in PIECES]
-        w_grouped = [picked_row[:, 3 * S + (r - 1) * QUARTER : 3 * S + r * QUARTER].bitcast(BF16) for r in range(2)]
+        w_grouped = [picked_row[:, c : c + QUARTER].bitcast(BF16) for c in (3 * S + HALF, 3 * S - P)]
         w_codes = [keep.tile([P, P], U32, name=f"w_codes{r}", align_bytes=64) for r in range(2)]
         w_scales = [keep.tile([P, P], U8, name=f"w_scales{r}", align_bytes=64) for r in range(2)]
         windows = [keep.tile([P, T], F32, name=f"window{r}") for r in range(2)]
@@ -134,8 +134,8 @@ def tile_list_hboth_silu_kernel(tc, xT, w, wgt, b, wgo, offs, offs2, out):
                 in_=grouped[n],
             )
 
-        def interleave_w(r):
-            nc.scalar.copy(
+        def interleave_w(copy, r):
+            copy(
                 w_grouped[r].rearrange("p (c j i) -> p c i j", j=4, i=PACK),
                 w_raw[:, :, r * P : (r + 1) * P].rearrange("p i (c j) -> p c i j", j=4),
             )
@@ -175,17 +175,18 @@ def tile_list_hboth_silu_kernel(tc, xT, w, wgt, b, wgo, offs, offs2, out):
         for n in range(2):
             interleave(0, n, *PIECES[n])
         gather(2, 0, S)
-        for c in (7 * P, 6 * P):
+        for c in (6 * P, 7 * P):
             gather(3, c, c + P)
             interleave(1, 0, c, c + P)
-        gather(3, QUARTER, 3 * QUARTER)
-        interleave_w(0)
-        interleave_w(1)
+        gather(3, QUARTER, HALF)
+        interleave_w(nc.vector.tensor_copy, 0)
+        interleave_w(nc.scalar.copy, 1)
         quantize(0)
         quantize_w(0)
         product(0, 0)
         quantize_w(1)
         product(1, 0)
+        gather(3, HALF, 3 * QUARTER)
         gather(3, 0, QUARTER)
         interleave(1, 1, *PIECES[1])
         scatter(0, y[0][0], *PIECES[0])

@@ -68,8 +68,9 @@ def tile_list_hboth_silu_kernel(tc, xT, w, wgt, b, wgo, offs, offs2, out):
 
         x_planes = xT.rearrange("(p i) t -> p i t", i=PACK)
         nc.sync.dma_start(rows[0:64, :], wgt[0:P:LIST_ROWS, :].rearrange("g (b c) -> b g c", c=P))
+        nc.sync.dma_start(planes[0][:], x_planes[:, 0, :])
         nc.sync.dma_start(offs_t[:], offs)
-        for i in range(PACK):
+        for i in range(1, PACK):
             nc.sync.dma_start(planes[i][:], x_planes[:, i, :])
 
         nc.vector.memset(warm[:], 0.0)
@@ -201,4 +202,7 @@ def tile_list_hboth_silu_kernel(tc, xT, w, wgt, b, wgo, offs, offs2, out):
             product(r, 2)
             product(r, 3)
             scatter(r, y_last[r][:], QUARTER, 3 * QUARTER)
-            nc.sync.dma_start(out[r * P : (r + 1) * P, :], windows[r][:])
+            if r == 0:
+                nc.sync.dma_start(out[0:P, :], windows[0][:])
+        nc.sync.dma_start(out[P:M, 0:S], windows[1][:, 0:S])
+        nc.scalar.dma_start(out[P:M, S:T], windows[1][:, S:T])

@@ -45,7 +45,10 @@ def tile_list_hboth_silu_kernel(tc, xT, w, wgt, b, wgo, offs, offs2, out):
         grouped = grouped + [late[r][:].bitcast(BF16) for r in range(2)]
         codes = [keep.tile([P, c1 - c0], U32, name=f"codes{c0}", align_bytes=64) for c0, c1 in PIECES]
         scales = [keep.tile([P, c1 - c0], U8, name=f"scales{c0}", align_bytes=64) for c0, c1 in PIECES]
-        w_grouped = [picked_row[:, c : c + QUARTER].bitcast(BF16) for c in (3 * S + HALF, 3 * S - P)]
+        w_grouped = [
+            keep.tile([P, P * PACK], BF16, name="w_first", align_bytes=64)[:],
+            picked_row[:, 3 * S - P : 3 * S + P].bitcast(BF16),
+        ]
         w_codes = [keep.tile([P, P], U32, name=f"w_codes{r}", align_bytes=64) for r in range(2)]
         w_scales = [keep.tile([P, P], U8, name=f"w_scales{r}", align_bytes=64) for r in range(2)]
         windows = [keep.tile([P, T], F32, name=f"window{r}") for r in range(2)]
@@ -64,13 +67,16 @@ def tile_list_hboth_silu_kernel(tc, xT, w, wgt, b, wgo, offs, offs2, out):
         ident = keep.tile([P, P], F32, name="ident")
         rows = keep.tile([P, P], F32, name="rows")
         spread = keep.tile([P, S], F32, name="spread")
-        w_raw = keep.tile([P, PACK, M], F32, name="w_raw")
+        w_raw = [keep.tile([P, PACK, P], F32, name=f"w_raw{r}") for r in range(2)]
 
         x_planes = xT.rearrange("(p i) t -> p i t", i=PACK)
         nc.sync.dma_start(rows[0:64, :], wgt[0:P:LIST_ROWS, :].rearrange("g (b c) -> b g c", c=P))
         nc.sync.dma_start(planes[0][:], x_planes[:, 0, :])
         nc.sync.dma_start(offs_t[:], offs)
+        w_rows = w.rearrange("(p i) m -> p i m", i=PACK)
         for i in range(1, PACK):
+            if i == PACK - 1:
+                nc.sync.dma_start(w_raw[0][:], w_rows[:, :, 0:P])
             nc.sync.dma_start(planes[i][:], x_planes[:, i, :])
 
         nc.vector.memset(warm[:], 0.0)
@@ -99,7 +105,7 @@ def tile_list_hboth_silu_kernel(tc, xT, w, wgt, b, wgo, offs, offs2, out):
                 nc.tensor.transpose(back[:, c : c + P], spread[:, c0 + c : c0 + c + P], ident[:])
             nc.scalar.copy(wgt_t[:, c0:c1], back[:])
 
-        nc.sync.dma_start(w_raw[:], w.rearrange("(p i) m -> p i m", i=PACK))
+        nc.sync.dma_start(w_raw[1][:], w_rows[:, :, P:M])
         with nc.allow_non_contiguous_dma(reason="bias, one value to a partition"):
             nc.sync.dma_start(b_t[:], b.rearrange("(r p) -> p r", p=P))
         nc.sync.dma_start(offs2_t[:], offs2)
@@ -138,7 +144,7 @@ def tile_list_hboth_silu_kernel(tc, xT, w, wgt, b, wgo, offs, offs2, out):
         def interleave_w(copy, r):
             copy(
                 w_grouped[r].rearrange("p (c j i) -> p c i j", j=4, i=PACK),
-                w_raw[:, :, r * P : (r + 1) * P].rearrange("p i (c j) -> p c i j", j=4),
+                w_raw[r][:].rearrange("p i (c j) -> p c i j", j=4),
             )
 
         def quantize_w(r):
@@ -175,19 +181,18 @@ def tile_list_hboth_silu_kernel(tc, xT, w, wgt, b, wgo, offs, offs2, out):
         gather(1, 0, S)
         for n in range(2):
             interleave(0, n, *PIECES[n])
+        interleave_w(nc.scalar.copy, 0)
         gather(2, 0, S)
+        quantize_w(0)
         for c in (6 * P, 7 * P):
             gather(3, c, c + P)
             interleave(1, 0, c, c + P)
-        gather(3, QUARTER, HALF)
-        interleave_w(nc.vector.tensor_copy, 0)
+        gather(3, QUARTER, 3 * QUARTER)
         interleave_w(nc.scalar.copy, 1)
         quantize(0)
-        quantize_w(0)
         product(0, 0)
         quantize_w(1)
         product(1, 0)
-        gather(3, HALF, 3 * QUARTER)
         gather(3, 0, QUARTER)
         interleave(1, 1, *PIECES[1])
         scatter(0, y[0][0], *PIECES[0])

@@ -20,10 +20,8 @@ PACK = 4
 HALF = S // 2
 QUARTER = S // 4
 LIST_ROWS = 16
-HEADS = P // LIST_ROWS
-SPREAD = ((0, 128), (128, 256), (256, 512), (512, 768), (768, 1024))
-BANK = ((7, 7), (1, 1), (2, 3), (4, 5))
-PIECES = ((768, 1024), (0, 256), (256, 512), (512, 768))
+A0, B0 = 3 * QUARTER, HALF
+X0 = 384
 
 
 def tile_list_hboth_silu_kernel(tc, xT, w, wgt, b, wgo, offs, offs2, out):
@@ -35,49 +33,44 @@ def tile_list_hboth_silu_kernel(tc, xT, w, wgt, b, wgo, offs, offs2, out):
         offs_t = keep.tile([P, S // LIST_ROWS], U16, name="offs_t")
         offs2_t = keep.tile([P, S // LIST_ROWS], U16, name="offs2_t")
         planes = [keep.tile([P, T], F32, name=f"plane{i}") for i in range(PACK)]
-        wgt_t = keep.tile([P, S], F32, name="wgt_t")
+        wgt_t = keep.tile([P, S], F32, name="wgt_t", align_bytes=64)
         wgo_t = keep.tile([P, S], F32, name="wgo_t")
         b_t = keep.tile([P, 2], F32, name="b_t")
         picked_row = keep.tile([P, PACK * S], F32, name="picked_row", align_bytes=64)
         picked = picked_row[:].rearrange("p (i n) -> p i n", i=PACK)
-        late = [keep.tile([P, HALF], F32, name=f"late{r}", align_bytes=64) for r in range(2)]
-        grouped = [keep.tile([P, (c1 - c0) * PACK], BF16, name=f"grouped{c0}", align_bytes=64)[:] for c0, c1 in PIECES[:2]]
-        grouped = grouped + [late[r][:].bitcast(BF16) for r in range(2)]
-        codes = [keep.tile([P, c1 - c0], U32, name=f"codes{c0}", align_bytes=64) for c0, c1 in PIECES]
-        scales = [keep.tile([P, c1 - c0], U8, name=f"scales{c0}", align_bytes=64) for c0, c1 in PIECES]
-        w_grouped = [
-            keep.tile([P, P * PACK], BF16, name="w_first", align_bytes=64)[:],
-            picked_row[:, 3 * S - P : 3 * S + P].bitcast(BF16),
-        ]
+        grouped_a = keep.tile([P, QUARTER * PACK], BF16, name="grouped_a", align_bytes=64)
+        grouped_b = keep.tile([P, QUARTER * PACK], BF16, name="grouped_b", align_bytes=64)
+        late = keep.tile([P, 2 * HALF], F32, name="late", align_bytes=64)
+        grouped_c = late[:].bitcast(BF16)
+        codes_ab = keep.tile([P, HALF], U32, name="codes_ab", align_bytes=64)
+        scales_ab = keep.tile([P, HALF], U8, name="scales_ab", align_bytes=64)
+        codes_c = keep.tile([P, HALF], U32, name="codes_c", align_bytes=64)
+        scales_c = keep.tile([P, HALF], U8, name="scales_c", align_bytes=64)
+        w_first = keep.tile([P, PACK * P], F32, name="w_first")
+        w_raw = [w_first[:], late[:, 0 : PACK * P]]
+        w_grouped = [wgt_t[:, A0:S].bitcast(BF16), grouped_b[:, 0 : PACK * P]]
         w_codes = [keep.tile([P, P], U32, name=f"w_codes{r}", align_bytes=64) for r in range(2)]
         w_scales = [keep.tile([P, P], U8, name=f"w_scales{r}", align_bytes=64) for r in range(2)]
         windows = [keep.tile([P, T], F32, name=f"window{r}") for r in range(2)]
-        y_second = [keep.tile([P, QUARTER], F32, name=f"y_second{r}") for r in range(2)]
-        y_last = [keep.tile([P, HALF], F32, name=f"y_last{r}") for r in range(2)]
-        y = [
-            [
-                late[r][:, 0:QUARTER],
-                y_second[r][:],
-                y_last[r][:, 0:QUARTER],
-                y_last[r][:, QUARTER:HALF],
-            ]
-            for r in range(2)
-        ]
+        y = [keep.tile([P, S], F32, name=f"y{r}") for r in range(2)]
         warm = keep.tile([P, 1], F32, name="warm")
         ident = keep.tile([P, P], F32, name="ident")
         rows = keep.tile([P, P], F32, name="rows")
         spread = keep.tile([P, S], F32, name="spread")
-        w_raw = [keep.tile([P, PACK, P], F32, name=f"w_raw{r}") for r in range(2)]
-
         x_planes = xT.rearrange("(p i) t -> p i t", i=PACK)
+        w_rows = w.rearrange("(p i) m -> p i m", i=PACK)
         nc.sync.dma_start(rows[0:64, :], wgt[0:P:LIST_ROWS, :].rearrange("g (b c) -> b g c", c=P))
         nc.sync.dma_start(planes[0][:], x_planes[:, 0, :])
         nc.sync.dma_start(offs_t[:], offs)
-        w_rows = w.rearrange("(p i) m -> p i m", i=PACK)
         for i in range(1, PACK):
-            if i == PACK - 1:
-                nc.sync.dma_start(w_raw[0][:], w_rows[:, :, 0:P])
             nc.sync.dma_start(planes[i][:], x_planes[:, i, :])
+        nc.sync.dma_start(w_raw[0].rearrange("p (i m) -> p i m", i=PACK), w_rows[:, :, 0:P])
+        with nc.allow_non_contiguous_dma(reason="bias, one value to a partition"):
+            nc.sync.dma_start(b_t[:], b.rearrange("(r p) -> p r", p=P))
+        nc.sync.dma_start(offs2_t[:], offs2)
+        nc.sync.dma_start(wgo_t[:, A0:S], wgo[:, A0:S])
+        nc.sync.dma_start(w_raw[1].rearrange("p (i m) -> p i m", i=PACK), w_rows[:, :, P:M])
+        nc.sync.dma_start(wgo_t[:, 0:A0], wgo[:, 0:A0])
 
         nc.vector.memset(warm[:], 0.0)
         nc.scalar.activation(warm[:], warm[:], SILU)
@@ -96,117 +89,95 @@ def tile_list_hboth_silu_kernel(tc, xT, w, wgt, b, wgo, offs, offs2, out):
                 turned[e][:, c0 // LIST_ROWS : c1 // LIST_ROWS].unsqueeze(2).to_broadcast([P, (c1 - c0) // LIST_ROWS, LIST_ROWS]),
             )
 
-        expand(nc.scalar.copy, 1, HALF, S)
-        for n, (c0, c1) in enumerate(SPREAD):
-            if c0 < HALF:
-                expand(nc.vector.tensor_copy, 0, c0, c1)
-            back = psum.tile([P, c1 - c0], F32, name=f"back{n}", tag=f"bk{n + 2}")
+        def turn_back(copy, bank, c0, c1):
+            back = psum.tile([P, c1 - c0], F32, name=f"back{bank}", tag=f"bk{bank}")
             for c in range(0, c1 - c0, P):
                 nc.tensor.transpose(back[:, c : c + P], spread[:, c0 + c : c0 + c + P], ident[:])
-            nc.scalar.copy(wgt_t[:, c0:c1], back[:])
+            copy(wgt_t[:, c0:c1], back[:])
 
-        nc.sync.dma_start(w_raw[1][:], w_rows[:, :, P:M])
-        with nc.allow_non_contiguous_dma(reason="bias, one value to a partition"):
-            nc.sync.dma_start(b_t[:], b.rearrange("(r p) -> p r", p=P))
-        nc.sync.dma_start(offs2_t[:], offs2)
-        nc.sync.dma_start(wgo_t[:, 3 * QUARTER : S], wgo[:, 3 * QUARTER : S])
-        nc.sync.dma_start(wgo_t[:, 0 : 3 * QUARTER], wgo[:, 0 : 3 * QUARTER])
+        expand(nc.vector.tensor_copy, 0, 0, QUARTER)
+        expand(nc.scalar.copy, 1, QUARTER, HALF)
+        expand(nc.scalar.copy, 1, HALF, S)
+        turn_back(nc.vector.tensor_copy, 2, 0, QUARTER)
+        turn_back(nc.scalar.copy, 3, QUARTER, HALF)
+        turn_back(nc.scalar.copy, 4, HALF, S)
 
-        def gather(i, c0, c1):
+        def gather(i, c0, c1, at):
             nc.vector.tensor_tensor(
-                picked_row[:, i * S + c0 : i * S + c1],
+                picked_row[:, at : at + c1 - c0],
                 planes[i][:].indirect(offs_t[:, c0 // LIST_ROWS : c1 // LIST_ROWS]),
                 wgt_t[:, c0:c1],
                 MULT,
             )
 
-        def interleave(pair, n, c0, c1):
-            first = PIECES[n][0]
+        def interleave_pair(grouped, pair, values):
             nc.scalar.copy(
-                grouped[n].rearrange("p (n i) -> p n i", i=PACK)[:, c0 - first : c1 - first, 2 * pair : 2 * pair + 2],
-                picked[:, 2 * pair : 2 * pair + 2, c0:c1].rearrange("p i n -> p n i"),
+                grouped.rearrange("p (n i) -> p n i", i=PACK)[:, :, 2 * pair : 2 * pair + 2],
+                values.rearrange("p i n -> p n i"),
             )
 
-        def interleave_all(n):
-            c0, c1 = PIECES[n]
-            nc.scalar.copy(
-                grouped[n].rearrange("p (c j i) -> p c i j", j=4, i=PACK),
-                picked[:, :, c0:c1].rearrange("p i (c j) -> p c i j", j=4),
-            )
-
-        def quantize(n):
-            nc.vector.quantize_mx(
-                out=codes[n][:].bitcast(FP8X4),
-                scales=scales[n][:],
-                in_=grouped[n],
-            )
-
-        def interleave_w(copy, r):
+        def interleave(copy, grouped, values):
             copy(
-                w_grouped[r].rearrange("p (c j i) -> p c i j", j=4, i=PACK),
-                w_raw[r][:].rearrange("p i (c j) -> p c i j", j=4),
+                grouped.rearrange("p (c j i) -> p c i j", j=4, i=PACK),
+                values.rearrange("p i (c j) -> p c i j", j=4),
             )
 
-        def quantize_w(r):
-            nc.vector.quantize_mx(
-                out=w_codes[r][:].bitcast(FP8X4),
-                scales=w_scales[r][:],
-                in_=w_grouped[r],
-            )
+        def quantize(codes, scales, grouped):
+            nc.vector.quantize_mx(out=codes.bitcast(FP8X4), scales=scales, in_=grouped)
 
-        def product(r, n):
-            c0, c1 = PIECES[n]
-            bank = psum.tile([P, c1 - c0], F32, name=f"bank{r}_{n}", tag=f"bk{BANK[n][r]}")
+        def product(r, codes, scales, c0, c1, bank):
+            acc = psum.tile([P, c1 - c0], F32, name=f"acc{r}_{c0}", tag=f"bk{bank}")
             nc.tensor.matmul_mx(
-                out=bank[:],
+                out=acc[:],
                 lhsT=w_codes[r][:].bitcast(FP8X4),
                 lhsT_scale=w_scales[r][:],
-                rhs=codes[n][:].bitcast(FP8X4),
-                rhs_scale=scales[n][:],
+                rhs=codes.bitcast(FP8X4),
+                rhs_scale=scales,
                 start=True,
                 stop=True,
             )
-            nc.scalar.activation(y[r][n], bank[:], SILU, bias=b_t[:, r : r + 1])
+            nc.scalar.activation(y[r][:, c0:c1], acc[:], SILU, bias=b_t[:, r : r + 1])
 
-        def scatter(r, values, c0, c1):
+        def scatter(r, c0, c1):
             nc.vector.tensor_tensor(
                 windows[r][:].indirect(offs2_t[:, c0 // LIST_ROWS : c1 // LIST_ROWS]),
-                values,
+                y[r][:, c0:c1],
                 wgo_t[:, c0:c1],
                 MULT,
             )
 
-        for c0, c1 in SPREAD:
-            gather(0, c0, c1)
-        gather(1, 0, S)
-        for n in range(2):
-            interleave(0, n, *PIECES[n])
-        interleave_w(nc.scalar.copy, 0)
-        gather(2, 0, S)
-        quantize_w(0)
-        for c in (6 * P, 7 * P):
-            gather(3, c, c + P)
-            interleave(1, 0, c, c + P)
-        gather(3, QUARTER, 3 * QUARTER)
-        interleave_w(nc.scalar.copy, 1)
-        quantize(0)
-        product(0, 0)
-        quantize_w(1)
-        product(1, 0)
-        gather(3, 0, QUARTER)
-        interleave(1, 1, *PIECES[1])
-        scatter(0, y[0][0], *PIECES[0])
-        quantize(1)
-        scatter(1, y[1][0], *PIECES[0])
+        def w_planes(r):
+            return w_raw[r].rearrange("p (i m) -> p i m", i=PACK)
+
+        gather(0, 0, QUARTER, 0)
+        gather(0, QUARTER, HALF, QUARTER)
+        gather(0, HALF, S, HALF)
+        gather(1, 0, S, S)
+        interleave_pair(grouped_a[:], 0, picked[:, 0:2, A0:S])
+        interleave_pair(grouped_b[:], 0, picked[:, 0:2, B0:A0])
+        gather(2, 0, S, 2 * S)
+        gather(3, A0, S, 3 * S)
+        gather(3, X0, A0, 3 * S + X0)
+        interleave_pair(grouped_a[:], 1, picked_row[:, 2 * S + A0 : 3 * S + QUARTER].rearrange("p (i n) -> p i n", i=2))
+        interleave(nc.vector.tensor_copy, w_grouped[0], w_planes(0))
+        interleave_pair(grouped_b[:], 1, picked[:, 2:4, B0:A0])
+        quantize(codes_ab[:, QUARTER:HALF], scales_ab[:, QUARTER:HALF], grouped_a[:])
+        quantize(w_codes[0][:], w_scales[0][:], w_grouped[0])
+        gather(3, 0, X0, 3 * S)
+        product(0, codes_ab[:, QUARTER:HALF], scales_ab[:, QUARTER:HALF], A0, S, 5)
+        quantize(codes_ab[:, 0:QUARTER], scales_ab[:, 0:QUARTER], grouped_b[:])
+        scatter(0, A0, S)
+        interleave(nc.scalar.copy, w_grouped[1], w_planes(1))
+        product(0, codes_ab[:, 0:QUARTER], scales_ab[:, 0:QUARTER], B0, A0, 6)
+        quantize(w_codes[1][:], w_scales[1][:], w_grouped[1])
+        scatter(0, B0, A0)
+        interleave(nc.scalar.copy, grouped_c, picked[:, :, 0:HALF])
+        product(1, codes_ab[:], scales_ab[:], B0, S, 7)
+        quantize(codes_c[:], scales_c[:], grouped_c)
+        scatter(1, B0, S)
         for r in range(2):
-            interleave_all(2 + r)
-            quantize(2 + r)
-            product(r, 1)
-            scatter(r, y[r][1], *PIECES[1])
-        for r in range(2):
-            product(r, 2)
-            product(r, 3)
-            scatter(r, y_last[r][:], QUARTER, 3 * QUARTER)
+            product(r, codes_c[:], scales_c[:], 0, HALF, r)
+            scatter(r, 0, HALF)
             if r == 0:
                 nc.sync.dma_start(out[0:P, :], windows[0][:])
         nc.sync.dma_start(out[P:M, 0:S], windows[1][:, 0:S])

@@ -21,6 +21,7 @@ HALF = S // 2
 QUARTER = S // 4
 LIST_ROWS = 16
 A0, B0 = 3 * QUARTER, HALF
+SPREAD = ((0, 128), (128, 384), (384, 640), (640, 1024))
 X0 = 384
 
 
@@ -48,7 +49,8 @@ def tile_list_hboth_silu_kernel(tc, xT, w, wgt, b, wgo, offs, offs2, out):
         scales_c = keep.tile([P, HALF], U8, name="scales_c", align_bytes=64)
         w_first = keep.tile([P, PACK * P], F32, name="w_first")
         w_raw = [w_first[:], late[:, 0 : PACK * P]]
-        w_grouped = [wgt_t[:, A0:S].bitcast(BF16), grouped_b[:, 0 : PACK * P]]
+        w_early = w_raw[0][:, 0 : 2 * P].rearrange("p (i m) -> p i m", i=2)
+        w_grouped = [picked_row[:, B0:A0].bitcast(BF16), grouped_b[:, 0 : PACK * P]]
         w_codes = [keep.tile([P, P], U32, name=f"w_codes{r}", align_bytes=64) for r in range(2)]
         w_scales = [keep.tile([P, P], U8, name=f"w_scales{r}", align_bytes=64) for r in range(2)]
         windows = [keep.tile([P, T], F32, name=f"window{r}") for r in range(2)]
@@ -63,8 +65,10 @@ def tile_list_hboth_silu_kernel(tc, xT, w, wgt, b, wgo, offs, offs2, out):
         nc.sync.dma_start(planes[0][:], x_planes[:, 0, :])
         nc.sync.dma_start(offs_t[:], offs)
         for i in range(1, PACK):
+            if i == PACK - 1:
+                nc.sync.dma_start(w_early, w_rows[:, 0:2, 0:P])
             nc.sync.dma_start(planes[i][:], x_planes[:, i, :])
-        nc.sync.dma_start(w_raw[0].rearrange("p (i m) -> p i m", i=PACK), w_rows[:, :, 0:P])
+        nc.sync.dma_start(w_raw[0][:, 2 * P : PACK * P].rearrange("p (i m) -> p i m", i=2), w_rows[:, 2:PACK, 0:P])
         with nc.allow_non_contiguous_dma(reason="bias, one value to a partition"):
             nc.sync.dma_start(b_t[:], b.rearrange("(r p) -> p r", p=P))
         nc.sync.dma_start(offs2_t[:], offs2)
@@ -95,12 +99,11 @@ def tile_list_hboth_silu_kernel(tc, xT, w, wgt, b, wgo, offs, offs2, out):
                 nc.tensor.transpose(back[:, c : c + P], spread[:, c0 + c : c0 + c + P], ident[:])
             copy(wgt_t[:, c0:c1], back[:])
 
-        expand(nc.vector.tensor_copy, 0, 0, QUARTER)
-        expand(nc.scalar.copy, 1, QUARTER, HALF)
-        expand(nc.scalar.copy, 1, HALF, S)
-        turn_back(nc.vector.tensor_copy, 2, 0, QUARTER)
-        turn_back(nc.scalar.copy, 3, QUARTER, HALF)
-        turn_back(nc.scalar.copy, 4, HALF, S)
+        expand(nc.vector.tensor_copy, 0, *SPREAD[0])
+        expand(nc.vector.tensor_copy, 0, *SPREAD[1])
+        expand(nc.scalar.copy, 1, SPREAD[2][0], S)
+        for n, (c0, c1) in enumerate(SPREAD):
+            turn_back(nc.vector.tensor_copy if n == 0 else nc.scalar.copy, n + 2, c0, c1)
 
         def gather(i, c0, c1, at):
             nc.vector.tensor_tensor(
@@ -149,30 +152,29 @@ def tile_list_hboth_silu_kernel(tc, xT, w, wgt, b, wgo, offs, offs2, out):
         def w_planes(r):
             return w_raw[r].rearrange("p (i m) -> p i m", i=PACK)
 
-        gather(0, 0, QUARTER, 0)
-        gather(0, QUARTER, HALF, QUARTER)
-        gather(0, HALF, S, HALF)
+        for c0, c1 in SPREAD:
+            gather(0, c0, c1, c0)
         gather(1, 0, S, S)
-        interleave_pair(grouped_a[:], 0, picked[:, 0:2, A0:S])
         interleave_pair(grouped_b[:], 0, picked[:, 0:2, B0:A0])
+        interleave_pair(grouped_a[:], 0, picked[:, 0:2, A0:S])
         gather(2, 0, S, 2 * S)
+        interleave(nc.scalar.copy, w_grouped[0], w_planes(0))
         gather(3, A0, S, 3 * S)
         gather(3, X0, A0, 3 * S + X0)
         interleave_pair(grouped_a[:], 1, picked_row[:, 2 * S + A0 : 3 * S + QUARTER].rearrange("p (i n) -> p i n", i=2))
-        interleave(nc.vector.tensor_copy, w_grouped[0], w_planes(0))
+        quantize(w_codes[0][:], w_scales[0][:], w_grouped[0])
         interleave_pair(grouped_b[:], 1, picked[:, 2:4, B0:A0])
         quantize(codes_ab[:, QUARTER:HALF], scales_ab[:, QUARTER:HALF], grouped_a[:])
-        quantize(w_codes[0][:], w_scales[0][:], w_grouped[0])
         gather(3, 0, X0, 3 * S)
-        product(0, codes_ab[:, QUARTER:HALF], scales_ab[:, QUARTER:HALF], A0, S, 5)
+        product(0, codes_ab[:, QUARTER:HALF], scales_ab[:, QUARTER:HALF], A0, S, 6)
         quantize(codes_ab[:, 0:QUARTER], scales_ab[:, 0:QUARTER], grouped_b[:])
         scatter(0, A0, S)
         interleave(nc.scalar.copy, w_grouped[1], w_planes(1))
-        product(0, codes_ab[:, 0:QUARTER], scales_ab[:, 0:QUARTER], B0, A0, 6)
+        product(0, codes_ab[:, 0:QUARTER], scales_ab[:, 0:QUARTER], B0, A0, 7)
         quantize(w_codes[1][:], w_scales[1][:], w_grouped[1])
         scatter(0, B0, A0)
         interleave(nc.scalar.copy, grouped_c, picked[:, :, 0:HALF])
-        product(1, codes_ab[:], scales_ab[:], B0, S, 7)
+        product(1, codes_ab[:], scales_ab[:], B0, S, 2)
         quantize(codes_c[:], scales_c[:], grouped_c)
         scatter(1, B0, S)
         for r in range(2):

@@ -22,7 +22,7 @@ QUARTER = S // 4
 LIST_ROWS = 16
 A0, B0 = 3 * QUARTER, HALF
 SPREAD = ((0, 128), (128, 384), (384, 640), (640, 1024))
-X0 = 384
+X0 = 512
 
 
 def tile_list_hboth_silu_kernel(tc, xT, w, wgt, b, wgo, offs, offs2, out):
@@ -159,9 +159,11 @@ def tile_list_hboth_silu_kernel(tc, xT, w, wgt, b, wgo, offs, offs2, out):
         interleave_pair(grouped_a[:], 0, picked[:, 0:2, A0:S])
         gather(2, 0, S, 2 * S)
         interleave(nc.scalar.copy, w_grouped[0], w_planes(0))
-        gather(3, A0, S, 3 * S)
+        last_pair = picked_row[:, 2 * S + A0 : 3 * S + QUARTER].rearrange("p (i n) -> p i n", i=2)
+        for c in (0, P):
+            gather(3, A0 + c, A0 + c + P, 3 * S + c)
+            interleave_pair(grouped_a[:, PACK * c : PACK * (c + P)], 1, last_pair[:, :, c : c + P])
         gather(3, X0, A0, 3 * S + X0)
-        interleave_pair(grouped_a[:], 1, picked_row[:, 2 * S + A0 : 3 * S + QUARTER].rearrange("p (i n) -> p i n", i=2))
         quantize(w_codes[0][:], w_scales[0][:], w_grouped[0])
         interleave_pair(grouped_b[:], 1, picked[:, 2:4, B0:A0])
         quantize(codes_ab[:, QUARTER:HALF], scales_ab[:, QUARTER:HALF], grouped_a[:])

@@ -158,7 +158,8 @@ def tile_list_hboth_silu_kernel(tc, xT, w, wgt, b, wgo, offs, offs2, out):
         interleave_pair(grouped_b[:], 0, picked[:, 0:2, B0:A0])
         interleave_pair(grouped_a[:], 0, picked[:, 0:2, A0:S])
         gather(2, 0, S, 2 * S)
-        interleave(nc.scalar.copy, w_grouped[0], w_planes(0))
+        for pair in range(2):
+            interleave_pair(w_grouped[0], pair, w_planes(0)[:, 2 * pair : 2 * pair + 2, :])
         last_pair = picked_row[:, 2 * S + A0 : 3 * S + QUARTER].rearrange("p (i n) -> p i n", i=2)
         for c in (0, P):
             gather(3, A0 + c, A0 + c + P, 3 * S + c)

@@ -21,7 +21,8 @@ HALF = S // 2
 QUARTER = S // 4
 LIST_ROWS = 16
 A0, B0 = 3 * QUARTER, HALF
-SPREAD = ((0, 128), (128, 384), (384, 640), (640, 1024))
+SPREAD = ((0, 128), (128, 384), (384, 512), (512, 896), (896, 1024))
+FIRST = ((0, 128), (128, 512), (512, 1024))
 X0 = 512
 
 
@@ -152,7 +153,7 @@ def tile_list_hboth_silu_kernel(tc, xT, w, wgt, b, wgo, offs, offs2, out):
         def w_planes(r):
             return w_raw[r].rearrange("p (i m) -> p i m", i=PACK)
 
-        for c0, c1 in SPREAD:
+        for c0, c1 in FIRST:
             gather(0, c0, c1, c0)
         gather(1, 0, S, S)
         interleave_pair(grouped_b[:], 0, picked[:, 0:2, B0:A0])

@@ -23,7 +23,7 @@ LIST_ROWS = 16
 A0, B0 = 3 * QUARTER, HALF
 SPREAD = ((0, 128), (128, 384), (384, 512), (512, 896), (896, 1024))
 FIRST = ((0, 128), (128, 512), (512, 1024))
-X0 = 512
+X0 = 416
 
 
 def tile_list_hboth_silu_kernel(tc, xT, w, wgt, b, wgo, offs, offs2, out):
@@ -168,9 +168,11 @@ def tile_list_hboth_silu_kernel(tc, xT, w, wgt, b, wgo, offs, offs2, out):
         gather(3, X0, A0, 3 * S + X0)
         quantize(w_codes[0][:], w_scales[0][:], w_grouped[0])
         interleave_pair(grouped_b[:], 1, picked[:, 2:4, B0:A0])
-        quantize(codes_ab[:, QUARTER:HALF], scales_ab[:, QUARTER:HALF], grouped_a[:])
+        for c in (0, P):
+            at = slice(QUARTER + c, QUARTER + c + P)
+            quantize(codes_ab[:, at], scales_ab[:, at], grouped_a[:, PACK * c : PACK * (c + P)])
+            product(0, codes_ab[:, at], scales_ab[:, at], A0 + c, A0 + c + P, 5 + c // P)
         gather(3, 0, X0, 3 * S)
-        product(0, codes_ab[:, QUARTER:HALF], scales_ab[:, QUARTER:HALF], A0, S, 6)
         quantize(codes_ab[:, 0:QUARTER], scales_ab[:, 0:QUARTER], grouped_b[:])
         scatter(0, A0, S)
         interleave(nc.scalar.copy, w_grouped[1], w_planes(1))

@@ -23,7 +23,7 @@ LIST_ROWS = 16
 A0, B0 = 3 * QUARTER, HALF
 SPREAD = ((0, 128), (128, 384), (384, 512), (512, 896), (896, 1024))
 FIRST = ((0, 128), (128, 512), (512, 1024))
-X0 = 416
+X0 = 384
 
 
 def tile_list_hboth_silu_kernel(tc, xT, w, wgt, b, wgo, offs, offs2, out):

@@ -50,7 +50,6 @@ def tile_list_hboth_silu_kernel(tc, xT, w, wgt, b, wgo, offs, offs2, out):
         scales_c = keep.tile([P, HALF], U8, name="scales_c", align_bytes=64)
         w_first = keep.tile([P, PACK * P], F32, name="w_first")
         w_raw = [w_first[:], late[:, 0 : PACK * P]]
-        w_early = w_raw[0][:, 0 : 2 * P].rearrange("p (i m) -> p i m", i=2)
         w_grouped = [picked_row[:, B0:A0].bitcast(BF16), grouped_b[:, 0 : PACK * P]]
         w_codes = [keep.tile([P, P], U32, name=f"w_codes{r}", align_bytes=64) for r in range(2)]
         w_scales = [keep.tile([P, P], U8, name=f"w_scales{r}", align_bytes=64) for r in range(2)]
@@ -67,9 +66,9 @@ def tile_list_hboth_silu_kernel(tc, xT, w, wgt, b, wgo, offs, offs2, out):
         nc.sync.dma_start(offs_t[:], offs)
         for i in range(1, PACK):
             if i == PACK - 1:
-                nc.sync.dma_start(w_early, w_rows[:, 0:2, 0:P])
+                nc.sync.dma_start(w_raw[0][:, 0:P], w_rows[:, 0, 0:P])
             nc.sync.dma_start(planes[i][:], x_planes[:, i, :])
-        nc.sync.dma_start(w_raw[0][:, 2 * P : PACK * P].rearrange("p (i m) -> p i m", i=2), w_rows[:, 2:PACK, 0:P])
+        nc.sync.dma_start(w_raw[0][:, P : PACK * P].rearrange("p (i m) -> p i m", i=PACK - 1), w_rows[:, 1:PACK, 0:P])
         with nc.allow_non_contiguous_dma(reason="bias, one value to a partition"):
             nc.sync.dma_start(b_t[:], b.rearrange("(r p) -> p r", p=P))
         nc.sync.dma_start(offs2_t[:], offs2)
@@ -159,8 +158,11 @@ def tile_list_hboth_silu_kernel(tc, xT, w, wgt, b, wgo, offs, offs2, out):
         interleave_pair(grouped_b[:], 0, picked[:, 0:2, B0:A0])
         interleave_pair(grouped_a[:], 0, picked[:, 0:2, A0:S])
         gather(2, 0, S, 2 * S)
-        for pair in range(2):
-            interleave_pair(w_grouped[0], pair, w_planes(0)[:, 2 * pair : 2 * pair + 2, :])
+        for i0, i1 in ((0, 1), (1, PACK)):
+            nc.scalar.copy(
+                w_grouped[0].rearrange("p (c j i) -> p c i j", j=4, i=PACK)[:, :, i0:i1, :],
+                w_planes(0)[:, i0:i1, :].rearrange("p i (c j) -> p c i j", j=4),
+            )
         last_pair = picked_row[:, 2 * S + A0 : 3 * S + QUARTER].rearrange("p (i n) -> p i n", i=2)
         for c in (0, P):
             gather(3, A0 + c, A0 + c + P, 3 * S + c)

@@ -42,14 +42,15 @@ def tile_list_hboth_silu_kernel(tc, xT, w, wgt, b, wgo, offs, offs2, out):
         picked = picked_row[:].rearrange("p (i n) -> p i n", i=PACK)
         grouped_a = keep.tile([P, QUARTER * PACK], BF16, name="grouped_a", align_bytes=64)
         grouped_b = keep.tile([P, QUARTER * PACK], BF16, name="grouped_b", align_bytes=64)
-        late = keep.tile([P, 2 * HALF], F32, name="late", align_bytes=64)
-        grouped_c = late[:].bitcast(BF16)
+        late = keep.tile([P, PACK * P], F32, name="late", align_bytes=64)
+        grouped_c_t = keep.tile([P, HALF * PACK], BF16, name="grouped_c", align_bytes=64)
+        grouped_c = grouped_c_t[:]
         codes_ab = keep.tile([P, HALF], U32, name="codes_ab", align_bytes=64)
         scales_ab = keep.tile([P, HALF], U8, name="scales_ab", align_bytes=64)
         codes_c = keep.tile([P, HALF], U32, name="codes_c", align_bytes=64)
         scales_c = keep.tile([P, HALF], U8, name="scales_c", align_bytes=64)
         w_first = keep.tile([P, PACK * P], F32, name="w_first")
-        w_raw = [w_first[:], late[:, 0 : PACK * P]]
+        w_raw = [w_first[:], late[:]]
         w_grouped = [picked_row[:, B0:A0].bitcast(BF16), grouped_b[:, 0 : PACK * P]]
         w_codes = [keep.tile([P, P], U32, name=f"w_codes{r}", align_bytes=64) for r in range(2)]
         w_scales = [keep.tile([P, P], U8, name=f"w_scales{r}", align_bytes=64) for r in range(2)]
@@ -69,11 +70,11 @@ def tile_list_hboth_silu_kernel(tc, xT, w, wgt, b, wgo, offs, offs2, out):
                 nc.sync.dma_start(w_raw[0][:, 0:P], w_rows[:, 0, 0:P])
             nc.sync.dma_start(planes[i][:], x_planes[:, i, :])
         nc.sync.dma_start(w_raw[0][:, P : PACK * P].rearrange("p (i m) -> p i m", i=PACK - 1), w_rows[:, 1:PACK, 0:P])
+        nc.sync.dma_start(w_raw[1].rearrange("p (i m) -> p i m", i=PACK), w_rows[:, :, P:M])
         with nc.allow_non_contiguous_dma(reason="bias, one value to a partition"):
             nc.sync.dma_start(b_t[:], b.rearrange("(r p) -> p r", p=P))
         nc.sync.dma_start(offs2_t[:], offs2)
         nc.sync.dma_start(wgo_t[:, A0:S], wgo[:, A0:S])
-        nc.sync.dma_start(w_raw[1].rearrange("p (i m) -> p i m", i=PACK), w_rows[:, :, P:M])
         nc.sync.dma_start(wgo_t[:, 0:A0], wgo[:, 0:A0])
 
         nc.vector.memset(warm[:], 0.0)
@@ -125,6 +126,12 @@ def tile_list_hboth_silu_kernel(tc, xT, w, wgt, b, wgo, offs, offs2, out):
                 values.rearrange("p i (c j) -> p c i j", j=4),
             )
 
+        def interleave_planes(grouped, values, i0, i1):
+            nc.scalar.copy(
+                grouped.rearrange("p (c j i) -> p c i j", j=4, i=PACK)[:, :, i0:i1, :],
+                values[:, i0:i1, :].rearrange("p i (c j) -> p c i j", j=4),
+            )
+
         def quantize(codes, scales, grouped):
             nc.vector.quantize_mx(out=codes.bitcast(FP8X4), scales=scales, in_=grouped)
 
@@ -154,6 +161,7 @@ def tile_list_hboth_silu_kernel(tc, xT, w, wgt, b, wgo, offs, offs2, out):
 
         for c0, c1 in FIRST:
             gather(0, c0, c1, c0)
+        interleave_planes(grouped_c, picked[:, :, 0:HALF], 0, 1)
         gather(1, 0, S, S)
         interleave_pair(grouped_b[:], 0, picked[:, 0:2, B0:A0])
         interleave_pair(grouped_a[:], 0, picked[:, 0:2, A0:S])
@@ -177,13 +185,15 @@ def tile_list_hboth_silu_kernel(tc, xT, w, wgt, b, wgo, offs, offs2, out):
         gather(3, 0, X0, 3 * S)
         quantize(codes_ab[:, 0:QUARTER], scales_ab[:, 0:QUARTER], grouped_b[:])
         scatter(0, A0, S)
+        interleave_planes(grouped_c[:, 0:S], picked[:, :, 0:QUARTER], 1, PACK)
         interleave(nc.scalar.copy, w_grouped[1], w_planes(1))
         product(0, codes_ab[:, 0:QUARTER], scales_ab[:, 0:QUARTER], B0, A0, 7)
+        quantize(codes_c[:, 0:QUARTER], scales_c[:, 0:QUARTER], grouped_c[:, 0:S])
         quantize(w_codes[1][:], w_scales[1][:], w_grouped[1])
         scatter(0, B0, A0)
-        interleave(nc.scalar.copy, grouped_c, picked[:, :, 0:HALF])
+        interleave_planes(grouped_c[:, S : 2 * S], picked[:, :, QUARTER:HALF], 1, PACK)
         product(1, codes_ab[:], scales_ab[:], B0, S, 2)
-        quantize(codes_c[:], scales_c[:], grouped_c)
+        quantize(codes_c[:, QUARTER:HALF], scales_c[:, QUARTER:HALF], grouped_c[:, S : 2 * S])
         scatter(1, B0, S)
         for r in range(2):
             product(r, codes_c[:], scales_c[:], 0, HALF, r)

@@ -185,14 +185,15 @@ def tile_list_hboth_silu_kernel(tc, xT, w, wgt, b, wgo, offs, offs2, out):
         gather(3, 0, X0, 3 * S)
         quantize(codes_ab[:, 0:QUARTER], scales_ab[:, 0:QUARTER], grouped_b[:])
         scatter(0, A0, S)
-        interleave_planes(grouped_c[:, 0:S], picked[:, :, 0:QUARTER], 1, PACK)
+        interleave_planes(grouped_c[:, 0:HALF], picked[:, :, 0:P], 1, PACK)
         interleave(nc.scalar.copy, w_grouped[1], w_planes(1))
         product(0, codes_ab[:, 0:QUARTER], scales_ab[:, 0:QUARTER], B0, A0, 7)
-        quantize(codes_c[:, 0:QUARTER], scales_c[:, 0:QUARTER], grouped_c[:, 0:S])
+        quantize(codes_c[:, 0:P], scales_c[:, 0:P], grouped_c[:, 0:HALF])
         quantize(w_codes[1][:], w_scales[1][:], w_grouped[1])
         scatter(0, B0, A0)
-        interleave_planes(grouped_c[:, S : 2 * S], picked[:, :, QUARTER:HALF], 1, PACK)
+        interleave_planes(grouped_c[:, HALF : 2 * S], picked[:, :, P:HALF], 1, PACK)
         product(1, codes_ab[:], scales_ab[:], B0, S, 2)
+        quantize(codes_c[:, P:QUARTER], scales_c[:, P:QUARTER], grouped_c[:, HALF:S])
         quantize(codes_c[:, QUARTER:HALF], scales_c[:, QUARTER:HALF], grouped_c[:, S : 2 * S])
         scatter(1, B0, S)
         for r in range(2):

@@ -202,4 +202,4 @@ def tile_list_hboth_silu_kernel(tc, xT, w, wgt, b, wgo, offs, offs2, out):
             if r == 0:
                 nc.sync.dma_start(out[0:P, :], windows[0][:])
         nc.sync.dma_start(out[P:M, 0:S], windows[1][:, 0:S])
-        nc.scalar.dma_start(out[P:M, S:T], windows[1][:, S:T])
+        nc.sync.dma_start(out[P:M, S:T], windows[1][:, S:T])

@@ -193,8 +193,7 @@ def tile_list_hboth_silu_kernel(tc, xT, w, wgt, b, wgo, offs, offs2, out):
         scatter(0, B0, A0)
         interleave_planes(grouped_c[:, HALF : 2 * S], picked[:, :, P:HALF], 1, PACK)
         product(1, codes_ab[:], scales_ab[:], B0, S, 2)
-        quantize(codes_c[:, P:QUARTER], scales_c[:, P:QUARTER], grouped_c[:, HALF:S])
-        quantize(codes_c[:, QUARTER:HALF], scales_c[:, QUARTER:HALF], grouped_c[:, S : 2 * S])
+        quantize(codes_c[:, P:HALF], scales_c[:, P:HALF], grouped_c[:, HALF : 2 * S])
         scatter(1, B0, S)
         for r in range(2):
             product(r, codes_c[:], scales_c[:], 0, HALF, r)

@@ -200,5 +200,4 @@ def tile_list_hboth_silu_kernel(tc, xT, w, wgt, b, wgo, offs, offs2, out):
             scatter(r, 0, HALF)
             if r == 0:
                 nc.sync.dma_start(out[0:P, :], windows[0][:])
-        nc.sync.dma_start(out[P:M, 0:S], windows[1][:, 0:S])
-        nc.sync.dma_start(out[P:M, S:T], windows[1][:, S:T])
+        nc.sync.dma_start(out[P:M, :], windows[1][:])

@@ -70,11 +70,11 @@ def tile_list_hboth_silu_kernel(tc, xT, w, wgt, b, wgo, offs, offs2, out):
                 nc.sync.dma_start(w_raw[0][:, 0:P], w_rows[:, 0, 0:P])
             nc.sync.dma_start(planes[i][:], x_planes[:, i, :])
         nc.sync.dma_start(w_raw[0][:, P : PACK * P].rearrange("p (i m) -> p i m", i=PACK - 1), w_rows[:, 1:PACK, 0:P])
-        nc.sync.dma_start(w_raw[1].rearrange("p (i m) -> p i m", i=PACK), w_rows[:, :, P:M])
         with nc.allow_non_contiguous_dma(reason="bias, one value to a partition"):
             nc.sync.dma_start(b_t[:], b.rearrange("(r p) -> p r", p=P))
         nc.sync.dma_start(offs2_t[:], offs2)
         nc.sync.dma_start(wgo_t[:, A0:S], wgo[:, A0:S])
+        nc.sync.dma_start(w_raw[1].rearrange("p (i m) -> p i m", i=PACK), w_rows[:, :, P:M])
         nc.sync.dma_start(wgo_t[:, 0:A0], wgo[:, 0:A0])
 
         nc.vector.memset(warm[:], 0.0)

@@ -80,8 +80,10 @@ def tile_list_hboth_silu_kernel(tc, xT, w, wgt, b, wgo, offs, offs2, out):
         nc.vector.memset(warm[:], 0.0)
         nc.scalar.activation(warm[:], warm[:], SILU)
         make_identity(nc, ident[:])
+        nc.gpsimd.memset(windows[0][:, 1536:T], 0.0)
         nc.gpsimd.memset(rows[64:P, :], 0.0)
-        nc.vector.memset(windows[0][:], 0.0)
+        nc.vector.memset(windows[0][:, 0:769], 0.0)
+        nc.vector.memset(windows[0][:, 769:1536], 0.0)
         nc.gpsimd.memset(windows[1][:], 0.0)
 
         turned = [psum.tile([P, P], F32, name=f"turned{e}", tag=f"bk{e}") for e in range(2)]

@@ -58,11 +58,11 @@ def tile_list_hboth_silu_kernel(tc, xT, w, wgt, b, wgo, offs, offs2, out):
         y = [keep.tile([P, S], F32, name=f"y{r}") for r in range(2)]
         warm = keep.tile([P, 1], F32, name="warm")
         ident = keep.tile([P, P], F32, name="ident")
-        rows = keep.tile([P, P], F32, name="rows")
+        rows = keep.tile([P, 2 * P], F32, name="rows")
         spread = keep.tile([P, S], F32, name="spread")
         x_planes = xT.rearrange("(p i) t -> p i t", i=PACK)
         w_rows = w.rearrange("(p i) m -> p i m", i=PACK)
-        nc.sync.dma_start(rows[0:64, :], wgt[0:P:LIST_ROWS, :].rearrange("g (b c) -> b g c", c=P))
+        nc.sync.dma_start(rows[0:32, :], wgt[0:P:LIST_ROWS, :].rearrange("g (b c) -> g b c", c=2 * P))
         nc.sync.dma_start(planes[0][:], x_planes[:, 0, :])
         nc.sync.dma_start(offs_t[:], offs)
         for i in range(1, PACK):
@@ -80,21 +80,24 @@ def tile_list_hboth_silu_kernel(tc, xT, w, wgt, b, wgo, offs, offs2, out):
         nc.vector.memset(warm[:], 0.0)
         nc.scalar.activation(warm[:], warm[:], SILU)
         make_identity(nc, ident[:])
-        nc.gpsimd.memset(windows[0][:, 1536:T], 0.0)
+        nc.gpsimd.memset(windows[0][:, 1792:T], 0.0)
+        nc.gpsimd.memset(rows[32:64, :], 0.0)
         nc.gpsimd.memset(rows[64:P, :], 0.0)
-        nc.vector.memset(windows[0][:, 0:769], 0.0)
-        nc.vector.memset(windows[0][:, 769:1536], 0.0)
+        nc.vector.memset(windows[0][:, 0:897], 0.0)
+        nc.vector.memset(windows[0][:, 897:1792], 0.0)
         nc.gpsimd.memset(windows[1][:], 0.0)
 
-        turned = [psum.tile([P, P], F32, name=f"turned{e}", tag=f"bk{e}") for e in range(2)]
-        for e in range(2):
-            nc.tensor.transpose(turned[e][:], rows[:], ident[:])
+        turned_v = [psum.tile([P, P], F32, name=f"turned_v{h}", tag=f"bk{7 * h}") for h in range(2)]
+        turned_s = psum.tile([P, 2 * P], F32, name="turned_s", tag="bk1")
+        nc.tensor.transpose(turned_v[0][:], rows[:, 0:P], ident[:])
+        for h in (1, 0):
+            nc.tensor.transpose(turned_s[:, h * P : (h + 1) * P], rows[:, h * P : (h + 1) * P], ident[:])
+        nc.tensor.transpose(turned_v[1][:], rows[:, P : 2 * P], ident[:])
+        blocks = spread[:].rearrange("j (b h g q) -> j b h g q", b=4, h=2, g=8)
 
-        def expand(copy, e, c0, c1):
-            copy(
-                spread[:, c0:c1].rearrange("j (k q) -> j k q", q=LIST_ROWS),
-                turned[e][:, c0 // LIST_ROWS : c1 // LIST_ROWS].unsqueeze(2).to_broadcast([P, (c1 - c0) // LIST_ROWS, LIST_ROWS]),
-            )
+        def expand_one(copy, turned, b0, h):
+            source = turned[:, 0:32].rearrange("j (g b) -> j b g", g=8)[:, b0, :]
+            copy(blocks[:, b0, h, :, :], source.unsqueeze(2).to_broadcast([P, 8, LIST_ROWS]))
 
         def turn_back(copy, bank, c0, c1):
             back = psum.tile([P, c1 - c0], F32, name=f"back{bank}", tag=f"bk{bank}")
@@ -102,9 +105,12 @@ def tile_list_hboth_silu_kernel(tc, xT, w, wgt, b, wgo, offs, offs2, out):
                 nc.tensor.transpose(back[:, c : c + P], spread[:, c0 + c : c0 + c + P], ident[:])
             copy(wgt_t[:, c0:c1], back[:])
 
-        expand(nc.vector.tensor_copy, 0, *SPREAD[0])
-        expand(nc.vector.tensor_copy, 0, *SPREAD[1])
-        expand(nc.scalar.copy, 1, SPREAD[2][0], S)
+        expand_one(nc.vector.tensor_copy, turned_v[0][:], 0, 0)
+        expand_one(nc.vector.tensor_copy, turned_v[0][:], 1, 0)
+        expand_one(nc.vector.tensor_copy, turned_v[1][:], 0, 1)
+        expand_one(nc.scalar.copy, turned_s[:, P : 2 * P], 1, 1)
+        upper = turned_s[:].rearrange("j (h n) -> j h n", h=2)[:, :, 0:32].rearrange("j h (g b) -> j b h g", g=8)[:, 2:4, :, :]
+        nc.scalar.copy(blocks[:, 2:4, :, :, :], upper.unsqueeze(4).to_broadcast([P, 2, 2, 8, LIST_ROWS]))
         for n, (c0, c1) in enumerate(SPREAD):
             turn_back(nc.vector.tensor_copy if n == 0 else nc.scalar.copy, n + 2, c0, c1)
 

@@ -16,6 +16,8 @@ MULT = mybir.AluOpType.mult
 SILU = mybir.ActivationFunctionType.Silu
 
 P = 128
+REGION = 65536
+WIDTH = {F32: 4, U32: 4, BF16: 2, U16: 2, U8: 1}
 PACK = 4
 HALF = S // 2
 QUARTER = S // 4
@@ -32,34 +34,49 @@ def tile_list_hboth_silu_kernel(tc, xT, w, wgt, b, wgo, offs, offs2, out):
         keep = ctx.enter_context(tc.tile_pool(name="keep", bufs=1))
         psum = ctx.enter_context(tc.psum_pool(name="psum", bufs=1))
 
-        offs_t = keep.tile([P, S // LIST_ROWS], U16, name="offs_t")
-        offs2_t = keep.tile([P, S // LIST_ROWS], U16, name="offs2_t")
-        planes = [keep.tile([P, T], F32, name=f"plane{i}") for i in range(PACK)]
-        wgt_t = keep.tile([P, S], F32, name="wgt_t", align_bytes=64)
-        wgo_t = keep.tile([P, S], F32, name="wgo_t")
-        b_t = keep.tile([P, 2], F32, name="b_t")
-        picked_row = keep.tile([P, PACK * S], F32, name="picked_row", align_bytes=64)
+        free = [0]
+
+        def place(shape, dtype, name, region=None):
+            if region is not None:
+                free[0] = region * REGION
+            at = free[0]
+            free[0] = at + -(-shape[1] * WIDTH[dtype] // 256) * 256
+            return keep.tile(shape, dtype, name=name, offset=at, align_bytes=256)
+
+        offs_t = place([P, S // LIST_ROWS], U16, name="offs_t")
+        offs2_t = place([P, S // LIST_ROWS], U16, name="offs2_t")
+        plane0 = place([P, T], F32, name="plane0")
+        wgt_t = place([P, S], F32, name="wgt_t")
+        b_t = place([P, 2], F32, name="b_t")
+        picked_row = place([P, PACK * S], F32, name="picked_row")
         picked = picked_row[:].rearrange("p (i n) -> p i n", i=PACK)
-        grouped_a = keep.tile([P, QUARTER * PACK], BF16, name="grouped_a", align_bytes=64)
-        grouped_b = keep.tile([P, QUARTER * PACK], BF16, name="grouped_b", align_bytes=64)
-        late = keep.tile([P, PACK * P], F32, name="late", align_bytes=64)
-        grouped_c_t = keep.tile([P, HALF * PACK], BF16, name="grouped_c", align_bytes=64)
+        grouped_a = place([P, QUARTER * PACK], BF16, name="grouped_a")
+        grouped_b = place([P, QUARTER * PACK], BF16, name="grouped_b")
+        grouped_c_t = place([P, HALF * PACK], BF16, name="grouped_c")
         grouped_c = grouped_c_t[:]
-        codes_ab = keep.tile([P, HALF], U32, name="codes_ab", align_bytes=64)
-        scales_ab = keep.tile([P, HALF], U8, name="scales_ab", align_bytes=64)
-        codes_c = keep.tile([P, HALF], U32, name="codes_c", align_bytes=64)
-        scales_c = keep.tile([P, HALF], U8, name="scales_c", align_bytes=64)
-        w_first = keep.tile([P, PACK * P], F32, name="w_first")
+        codes_ab = place([P, HALF], U32, name="codes_ab")
+        scales_ab = place([P, HALF], U8, name="scales_ab")
+        codes_c = place([P, HALF], U32, name="codes_c")
+        scales_c = place([P, HALF], U8, name="scales_c")
+        w_codes = [place([P, P], U32, name=f"w_codes{r}") for r in range(2)]
+        w_scales = [place([P, P], U8, name=f"w_scales{r}") for r in range(2)]
+        warm = place([P, 1], F32, name="warm")
+        ident = place([P, P], F32, name="ident")
+        rows = place([P, 2 * P], F32, name="rows")
+        plane1 = place([P, T], F32, name="plane1", region=1)
+        wgo_t = place([P, S], F32, name="wgo_t")
+        late = place([P, PACK * P], F32, name="late")
+        w_first = place([P, PACK * P], F32, name="w_first")
         w_raw = [w_first[:], late[:]]
         w_grouped = [picked_row[:, B0:A0].bitcast(BF16), grouped_b[:, 0 : PACK * P]]
-        w_codes = [keep.tile([P, P], U32, name=f"w_codes{r}", align_bytes=64) for r in range(2)]
-        w_scales = [keep.tile([P, P], U8, name=f"w_scales{r}", align_bytes=64) for r in range(2)]
-        windows = [keep.tile([P, T], F32, name=f"window{r}") for r in range(2)]
-        y = [keep.tile([P, S], F32, name=f"y{r}") for r in range(2)]
-        warm = keep.tile([P, 1], F32, name="warm")
-        ident = keep.tile([P, P], F32, name="ident")
-        rows = keep.tile([P, 2 * P], F32, name="rows")
-        spread = keep.tile([P, S], F32, name="spread")
+        y = [place([P, S], F32, name=f"y{r}") for r in range(2)]
+        spread = place([P, S], F32, name="spread")
+        plane2 = place([P, T], F32, name="plane2", region=2)
+        window0 = place([P, T], F32, name="window0")
+        plane3 = place([P, T], F32, name="plane3", region=3)
+        window1 = place([P, T], F32, name="window1")
+        planes = [plane0, plane1, plane2, plane3]
+        windows = [window0, window1]
         x_planes = xT.rearrange("(p i) t -> p i t", i=PACK)
         w_rows = w.rearrange("(p i) m -> p i m", i=PACK)
         nc.sync.dma_start(rows[0:32, :], wgt[0:P:LIST_ROWS, :].rearrange("g (b c) -> g b c", c=2 * P))
@@ -89,10 +106,10 @@ def tile_list_hboth_silu_kernel(tc, xT, w, wgt, b, wgo, offs, offs2, out):
 
         turned_v = [psum.tile([P, P], F32, name=f"turned_v{h}", tag=f"bk{7 * h}") for h in range(2)]
         turned_s = psum.tile([P, 2 * P], F32, name="turned_s", tag="bk1")
-        nc.tensor.transpose(turned_v[0][:], rows[:, 0:P], ident[:])
-        for h in (1, 0):
+        for h in range(2):
+            nc.tensor.transpose(turned_v[h][:], rows[:, h * P : (h + 1) * P], ident[:])
+        for h in range(2):
             nc.tensor.transpose(turned_s[:, h * P : (h + 1) * P], rows[:, h * P : (h + 1) * P], ident[:])
-        nc.tensor.transpose(turned_v[1][:], rows[:, P : 2 * P], ident[:])
         blocks = spread[:].rearrange("j (b h g q) -> j b h g q", b=4, h=2, g=8)
 
         def expand_one(copy, turned, b0, h):
@@ -106,9 +123,9 @@ def tile_list_hboth_silu_kernel(tc, xT, w, wgt, b, wgo, offs, offs2, out):
             copy(wgt_t[:, c0:c1], back[:])
 
         expand_one(nc.vector.tensor_copy, turned_v[0][:], 0, 0)
-        expand_one(nc.vector.tensor_copy, turned_v[0][:], 1, 0)
         expand_one(nc.vector.tensor_copy, turned_v[1][:], 0, 1)
-        expand_one(nc.scalar.copy, turned_s[:, P : 2 * P], 1, 1)
+        expand_one(nc.vector.tensor_copy, turned_v[0][:], 1, 0)
+        expand_one(nc.vector.tensor_copy, turned_v[1][:], 1, 1)
         upper = turned_s[:].rearrange("j (h n) -> j h n", h=2)[:, :, 0:32].rearrange("j h (g b) -> j b h g", g=8)[:, 2:4, :, :]
         nc.scalar.copy(blocks[:, 2:4, :, :, :], upper.unsqueeze(4).to_broadcast([P, 2, 2, 8, LIST_ROWS]))
         for n, (c0, c1) in enumerate(SPREAD):

from contextlib import ExitStack

import concourse.mybir as mybir
from concourse.masks import make_identity

K, M, T, S = 512, 256, 2048, 1024
FLOPS = 2 * K * M * S

F32 = mybir.dt.float32
BF16 = mybir.dt.bfloat16
U32 = mybir.dt.uint32
U16 = mybir.dt.uint16
U8 = mybir.dt.uint8
FP8X4 = mybir.dt.float8_e4m3fn_x4
MULT = mybir.AluOpType.mult
SILU = mybir.ActivationFunctionType.Silu

P = 128
REGION = 65536
WIDTH = {F32: 4, U32: 4, BF16: 2, U16: 2, U8: 1}
PACK = 4
HALF = S // 2
QUARTER = S // 4
LIST_ROWS = 16
A0, B0 = 3 * QUARTER, HALF
SPREAD = ((0, 128), (128, 384), (384, 512), (512, 896), (896, 1024))
FIRST = ((0, 128), (128, 512), (512, 1024))
X0 = 384


def tile_list_hboth_silu_kernel(tc, xT, w, wgt, b, wgo, offs, offs2, out):
    nc = tc.nc
    with ExitStack() as ctx:
        keep = ctx.enter_context(tc.tile_pool(name="keep", bufs=1))
        psum = ctx.enter_context(tc.psum_pool(name="psum", bufs=1))

        free = [0]

        def place(shape, dtype, name, region=None):
            if region is not None:
                free[0] = region * REGION
            at = free[0]
            free[0] = at + -(-shape[1] * WIDTH[dtype] // 256) * 256
            return keep.tile(shape, dtype, name=name, offset=at, align_bytes=256)

        offs_t = place([P, S // LIST_ROWS], U16, name="offs_t")
        offs2_t = place([P, S // LIST_ROWS], U16, name="offs2_t")
        plane0 = place([P, T], F32, name="plane0")
        wgt_t = place([P, S], F32, name="wgt_t")
        b_t = place([P, 2], F32, name="b_t")
        picked_row = place([P, PACK * S], F32, name="picked_row")
        picked = picked_row[:].rearrange("p (i n) -> p i n", i=PACK)
        grouped_a = place([P, QUARTER * PACK], BF16, name="grouped_a")
        grouped_b = place([P, QUARTER * PACK], BF16, name="grouped_b")
        grouped_c_t = place([P, HALF * PACK], BF16, name="grouped_c")
        grouped_c = grouped_c_t[:]
        codes_ab = place([P, HALF], U32, name="codes_ab")
        scales_ab = place([P, HALF], U8, name="scales_ab")
        codes_c = place([P, HALF], U32, name="codes_c")
        scales_c = place([P, HALF], U8, name="scales_c")
        w_codes = [place([P, P], U32, name=f"w_codes{r}") for r in range(2)]
        w_scales = [place([P, P], U8, name=f"w_scales{r}") for r in range(2)]
        warm = place([P, 1], F32, name="warm")
        ident = place([P, P], F32, name="ident")
        rows = place([P, 2 * P], F32, name="rows")
        plane1 = place([P, T], F32, name="plane1", region=1)
        wgo_t = place([P, S], F32, name="wgo_t")
        late = place([P, PACK * P], F32, name="late")
        w_first = place([P, PACK * P], F32, name="w_first")
        w_raw = [w_first[:], late[:]]
        w_grouped = [picked_row[:, B0:A0].bitcast(BF16), grouped_b[:, 0 : PACK * P]]
        y = [place([P, S], F32, name=f"y{r}") for r in range(2)]
        spread = place([P, S], F32, name="spread")
        plane2 = place([P, T], F32, name="plane2", region=2)
        window0 = place([P, T], F32, name="window0")
        plane3 = place([P, T], F32, name="plane3", region=3)
        window1 = place([P, T], F32, name="window1")
        planes = [plane0, plane1, plane2, plane3]
        windows = [window0, window1]
        x_planes = xT.rearrange("(p i) t -> p i t", i=PACK)
        w_rows = w.rearrange("(p i) m -> p i m", i=PACK)
        nc.sync.dma_start(rows[0:32, :], wgt[0:P:LIST_ROWS, :].rearrange("g (b c) -> g b c", c=2 * P))
        nc.sync.dma_start(planes[0][:], x_planes[:, 0, :])
        nc.sync.dma_start(offs_t[:], offs)
        for i in range(1, PACK):
            if i == PACK - 1:
                nc.sync.dma_start(w_raw[0][:, 0:P], w_rows[:, 0, 0:P])
            nc.sync.dma_start(planes[i][:], x_planes[:, i, :])
        nc.sync.dma_start(w_raw[0][:, P : PACK * P].rearrange("p (i m) -> p i m", i=PACK - 1), w_rows[:, 1:PACK, 0:P])
        with nc.allow_non_contiguous_dma(reason="bias, one value to a partition"):
            nc.sync.dma_start(b_t[:], b.rearrange("(r p) -> p r", p=P))
        nc.sync.dma_start(offs2_t[:], offs2)
        nc.sync.dma_start(wgo_t[:, A0:S], wgo[:, A0:S])
        nc.sync.dma_start(w_raw[1].rearrange("p (i m) -> p i m", i=PACK), w_rows[:, :, P:M])
        nc.sync.dma_start(wgo_t[:, 0:A0], wgo[:, 0:A0])

        nc.vector.memset(warm[:], 0.0)
        nc.scalar.activation(warm[:], warm[:], SILU)
        make_identity(nc, ident[:])
        nc.gpsimd.memset(windows[0][:, 1792:T], 0.0)
        nc.gpsimd.memset(rows[32:64, :], 0.0)
        nc.gpsimd.memset(rows[64:P, :], 0.0)
        nc.vector.memset(windows[0][:, 0:897], 0.0)
        nc.vector.memset(windows[0][:, 897:1792], 0.0)
        nc.gpsimd.memset(windows[1][:], 0.0)

        turned_v = [psum.tile([P, P], F32, name=f"turned_v{h}", tag=f"bk{7 * h}") for h in range(2)]
        turned_s = psum.tile([P, 2 * P], F32, name="turned_s", tag="bk1")
        for h in range(2):
            nc.tensor.transpose(turned_v[h][:], rows[:, h * P : (h + 1) * P], ident[:])
        for h in range(2):
            nc.tensor.transpose(turned_s[:, h * P : (h + 1) * P], rows[:, h * P : (h + 1) * P], ident[:])
        blocks = spread[:].rearrange("j (b h g q) -> j b h g q", b=4, h=2, g=8)

        def expand_one(copy, turned, b0, h):
            source = turned[:, 0:32].rearrange("j (g b) -> j b g", g=8)[:, b0, :]
            copy(blocks[:, b0, h, :, :], source.unsqueeze(2).to_broadcast([P, 8, LIST_ROWS]))

        def turn_back(copy, bank, c0, c1):
            back = psum.tile([P, c1 - c0], F32, name=f"back{bank}", tag=f"bk{bank}")
            for c in range(0, c1 - c0, P):
                nc.tensor.transpose(back[:, c : c + P], spread[:, c0 + c : c0 + c + P], ident[:])
            copy(wgt_t[:, c0:c1], back[:])

        expand_one(nc.vector.tensor_copy, turned_v[0][:], 0, 0)
        expand_one(nc.vector.tensor_copy, turned_v[1][:], 0, 1)
        expand_one(nc.vector.tensor_copy, turned_v[0][:], 1, 0)
        expand_one(nc.vector.tensor_copy, turned_v[1][:], 1, 1)
        upper = turned_s[:].rearrange("j (h n) -> j h n", h=2)[:, :, 0:32].rearrange("j h (g b) -> j b h g", g=8)[:, 2:4, :, :]
        nc.scalar.copy(blocks[:, 2:4, :, :, :], upper.unsqueeze(4).to_broadcast([P, 2, 2, 8, LIST_ROWS]))
        for n, (c0, c1) in enumerate(SPREAD):
            turn_back(nc.vector.tensor_copy if n == 0 else nc.scalar.copy, n + 2, c0, c1)

        def gather(i, c0, c1, at):
            nc.vector.tensor_tensor(
                picked_row[:, at : at + c1 - c0],
                planes[i][:].indirect(offs_t[:, c0 // LIST_ROWS : c1 // LIST_ROWS]),
                wgt_t[:, c0:c1],
                MULT,
            )

        def interleave_pair(grouped, pair, values):
            nc.scalar.copy(
                grouped.rearrange("p (n i) -> p n i", i=PACK)[:, :, 2 * pair : 2 * pair + 2],
                values.rearrange("p i n -> p n i"),
            )

        def interleave(copy, grouped, values):
            copy(
                grouped.rearrange("p (c j i) -> p c i j", j=4, i=PACK),
                values.rearrange("p i (c j) -> p c i j", j=4),
            )

        def interleave_planes(grouped, values, i0, i1):
            nc.scalar.copy(
                grouped.rearrange("p (c j i) -> p c i j", j=4, i=PACK)[:, :, i0:i1, :],
                values[:, i0:i1, :].rearrange("p i (c j) -> p c i j", j=4),
            )

        def quantize(codes, scales, grouped):
            nc.vector.quantize_mx(out=codes.bitcast(FP8X4), scales=scales, in_=grouped)

        def product(r, codes, scales, c0, c1, bank):
            acc = psum.tile([P, c1 - c0], F32, name=f"acc{r}_{c0}", tag=f"bk{bank}")
            nc.tensor.matmul_mx(
                out=acc[:],
                lhsT=w_codes[r][:].bitcast(FP8X4),
                lhsT_scale=w_scales[r][:],
                rhs=codes.bitcast(FP8X4),
                rhs_scale=scales,
                start=True,
                stop=True,
            )
            nc.scalar.activation(y[r][:, c0:c1], acc[:], SILU, bias=b_t[:, r : r + 1])

        def scatter(r, c0, c1):
            nc.vector.tensor_tensor(
                windows[r][:].indirect(offs2_t[:, c0 // LIST_ROWS : c1 // LIST_ROWS]),
                y[r][:, c0:c1],
                wgo_t[:, c0:c1],
                MULT,
            )

        def w_planes(r):
            return w_raw[r].rearrange("p (i m) -> p i m", i=PACK)

        for c0, c1 in FIRST:
            gather(0, c0, c1, c0)
        interleave_planes(grouped_c, picked[:, :, 0:HALF], 0, 1)
        gather(1, 0, S, S)
        interleave_pair(grouped_b[:], 0, picked[:, 0:2, B0:A0])
        interleave_pair(grouped_a[:], 0, picked[:, 0:2, A0:S])
        gather(2, 0, S, 2 * S)
        for i0, i1 in ((0, 1), (1, PACK)):
            nc.scalar.copy(
                w_grouped[0].rearrange("p (c j i) -> p c i j", j=4, i=PACK)[:, :, i0:i1, :],
                w_planes(0)[:, i0:i1, :].rearrange("p i (c j) -> p c i j", j=4),
            )
        last_pair = picked_row[:, 2 * S + A0 : 3 * S + QUARTER].rearrange("p (i n) -> p i n", i=2)
        for c in (0, P):
            gather(3, A0 + c, A0 + c + P, 3 * S + c)
            interleave_pair(grouped_a[:, PACK * c : PACK * (c + P)], 1, last_pair[:, :, c : c + P])
        gather(3, X0, A0, 3 * S + X0)
        quantize(w_codes[0][:], w_scales[0][:], w_grouped[0])
        interleave_pair(grouped_b[:], 1, picked[:, 2:4, B0:A0])
        for c in (0, P):
            at = slice(QUARTER + c, QUARTER + c + P)
            quantize(codes_ab[:, at], scales_ab[:, at], grouped_a[:, PACK * c : PACK * (c + P)])
            product(0, codes_ab[:, at], scales_ab[:, at], A0 + c, A0 + c + P, 5 + c // P)
        gather(3, 0, X0, 3 * S)
        quantize(codes_ab[:, 0:QUARTER], scales_ab[:, 0:QUARTER], grouped_b[:])
        scatter(0, A0, S)
        interleave_planes(grouped_c[:, 0:HALF], picked[:, :, 0:P], 1, PACK)
        interleave(nc.scalar.copy, w_grouped[1], w_planes(1))
        product(0, codes_ab[:, 0:QUARTER], scales_ab[:, 0:QUARTER], B0, A0, 7)
        quantize(codes_c[:, 0:P], scales_c[:, 0:P], grouped_c[:, 0:HALF])
        quantize(w_codes[1][:], w_scales[1][:], w_grouped[1])
        scatter(0, B0, A0)
        interleave_planes(grouped_c[:, HALF : 2 * S], picked[:, :, P:HALF], 1, PACK)
        product(1, codes_ab[:], scales_ab[:], B0, S, 2)
        quantize(codes_c[:, P:HALF], scales_c[:, P:HALF], grouped_c[:, HALF : 2 * S])
        scatter(1, B0, S)
        for r in range(2):
            product(r, codes_c[:], scales_c[:], 0, HALF, r)
            scatter(r, 0, HALF)
            if r == 0:
                nc.sync.dma_start(out[0:P, :], windows[0][:])
        nc.sync.dma_start(out[P:M, :], windows[1][:])
